import numpy as np, ml_dtypes
CORES = [3,11,19,27,35,43,51,59]
N = 8
BF = ml_dtypes.bfloat16
def gentries(a):
    return np.ascontiguousarray(a.reshape(8, 16, -1).transpose(0, 2, 1)).reshape(8, -1)
def gtable(e):
    e = np.asarray(e); return np.ascontiguousarray(e.reshape(8, -1, 16).transpose(0, 2, 1)).reshape(128, -1).astype(np.int32)
P, S, H, C, D, TH = 1536, 128, 8192, 2, 4, 7040
W = P + (N - 1) * S
def stored(v):
    return np.stack([gtable(np.reshape(v[r], (8, -1))) for r in range(N)])
def setup_inputs(rng):
    v = rng.integers(0, 8, (N, 8, 16, P)) + rng.integers(32, 128, (N, 8, 1, P)) * (np.arange(16)[:, None] == rng.integers(0, 16, (N, 8, 1, P)))
    return {"x": v.reshape(N, 128, P).astype(np.float32).astype(BF), "sus": np.floor(256 * rng.random((N, 128, H)) ** 2).astype(np.float32).astype(BF),
            "hist": stored(rng.integers(0, H, (N, 8, P))), "home": stored(rng.integers(0, W, (N, 8, C, P))), "away": stored(rng.integers(0, W, (N, 8, C, P))),
            "shown": stored(rng.integers(0, P, (N, 8, N - 1, S)))}
def setup_inputs_ties(rng):
    d = setup_inputs(rng); b = TH // 64
    d["x"] = (64 * (rng.random((N, 128, P)) * C < 0.25)).astype(np.float32).astype(BF)
    d["sus"] = rng.choice(np.array([0, 0, b, b + 1]), (N, 128, H)).astype(np.float32).astype(BF); return d
def setup_inputs_ends(rng):
    d = setup_inputs(rng); e = np.array([0, P - 1] + [P + k * S for k in range(N - 1)] + [P + k * S + S - 1 for k in range(N - 1)])
    for a, w in (("home", e), ("away", e), ("shown", e[:2]), ("hist", np.array([0, 15, H - 16, H - 1]))):
        d[a] = np.where(rng.random(d[a].shape) < 0.5, rng.choice(w, d[a].shape), d[a]).astype(np.int32)
    return d
def setup_inputs_one(rng):
    d = setup_inputs(rng); o = np.ones((1, 1, P), np.int64)
    d["hist"] = stored(rng.integers(0, H, (N, 8, 1)) * o); d["home"] = stored(rng.integers(0, W, (N, 8, 1)) * np.ones((1, 1, C * P), np.int64)); return d
def setup_inputs_far(rng):
    d = setup_inputs(rng); own = rng.integers(0, P, (N, 8, C, P)); out = rng.integers(P, W, (N, 8, C, P)); even = (np.arange(N) % 2 == 0)[:, None, None, None]
    d["home"] = stored(np.where(even, out, own)); d["away"] = stored(np.where(even, own, out)); return d
def setup_inputs_spread(rng):
    d = setup_inputs(rng); s = np.where(rng.random((N, 8, 1, P)) < 0.5, rng.integers(0, 4, (N, 8, 1, P)), rng.integers(0, 9, (N, 8, 1, P)))
    d["x"] = np.floor(256 * rng.random((N, 8, 16, P)) * np.exp2(-s)).reshape(N, 128, P).astype(np.float32).astype(BF)
    d["sus"] = np.floor(256 * rng.random((N, 8, 16, H)) * np.exp2(-rng.integers(0, 6, (N, 8, 1, H)))).reshape(N, 128, H).astype(np.float32).astype(BF)
    for a, n, k in (("hist", H, P), ("home", W, C * P), ("away", W, C * P), ("shown", P, (N - 1) * S)):
        d[a] = stored((np.floor(n * rng.random((N, 8, k)) ** 3).astype(np.int64) + rng.integers(0, n, (N, 8, 1))) % n)
    return d
def check_inputs(d):
    bad = []
    for a in ("x", "sus"):
        v = d[a].astype(np.float32)
        if not ((v >= 0) & (v <= 255) & (v == np.floor(v))).all(): bad.append(a)
    for a, n in (("hist", H), ("home", W), ("away", W), ("shown", P)):
        if not ((d[a] >= 0) & (d[a] < n)).all(): bad.append(a)
    return bad
def reference(x, sus, hist, home, away, shown):
    load = x.astype(np.float32).astype(np.int64).reshape(N, 8, 16, P); tab = sus.astype(np.float32).astype(np.int64).reshape(N, 8, 16, H)
    code = np.stack([gentries(hist[r]) for r in range(N)]).astype(np.int64); ill = np.zeros((N, 8, P), bool)
    near = np.stack([gentries(home[r]) for r in range(N)]).reshape(N, 8, C, P); far = np.stack([gentries(away[r]) for r in range(N)]).reshape(N, 8, C, P)
    give = np.stack([gentries(shown[r]) for r in range(N)]).reshape(N, 8, N - 1, S)
    for day in range(D):
        new = load >> 1
        for r in range(N):
            parts = [load[r]]
            for q in range(N):
                if q != r: parts.append(np.take_along_axis(load[q], give[q][:, None, r if r < q else r - 1], 2))
            win = np.concatenate(parts, 2)
            con = np.where(ill[r][:, None], far[r], near[r]).reshape(8, 1, C * P)
            pressure = np.sum(np.take_along_axis(win, con, 2).reshape(8, 16, C, P), axis=2)
            score = pressure * np.take_along_axis(tab[r], code[r][:, None], 2)
            best = np.argmax(score, axis=1); hit = np.max(score, axis=1) > TH
            new[r] += 64 * ((np.arange(16)[:, None] == best[:, None]) & hit[:, None])
            code[r] = np.where(hit, (16 * code[r] + best) & (H - 1), code[r]); ill[r] = hit
        load = new
    return {"y": load.reshape(N, 128, P).astype(np.float32), "h": stored(code).astype(np.float32)}

@@ -1,0 +1,458 @@
+from concourse.bass import DstId, RemoteDMATransfer
+from concourse.mybir import AluOpType as Alu, ActivationFunctionType as Act
+
+N, P, S, H, DAYS, TH = 8, 1536, 128, 8192, 4, 7040
+W = P + (N - 1) * S
+NS = (N - 1) * S
+BLK = 128
+EARLY = 8
+PF = 384
+TAIL = "G0 G1 wl fl tl ll A0 v34 A1 O0 O1 cl H0 v46"
+CFG = {
+    "chunks": [(0, 2), (2, 4), (4, 6), (6, 8), (8, 10), (10, 12)],
+    "sren": [[(0, 384), (384, 768)], [(256, 512), (512, 768)]],
+    "first": "ps1 pv0 ps3 pv2 ps5 pv4 gv0 d0 gs1 T0 T1 gs2 kv0 T2 gs3 m0 kv1 T3 ks2 s0 gs4 m1 T4 h0 ks3 m2 gs5 s1 T5 ks4 "
+             "s2 m3 ks5 h1 s3 we m4 fe s4 te le m5 ce s5 " + TAIL,
+    "later": "ps1 pv0 K ps2 m1 m0 h0 ps3 s1 s0 m2 ps4 s2 m3 h1 Ps5 Z s3 we m4 fe s4 te le m5 ce s5 " + TAIL,
+    "last": "ps1 pv0 K ps2 m1 m0 h0 ps3 s1 s0 wa m2 fa ps4 s2 ta la m3 ca h1 Ps5 s3 v01 G0 A0 O0 Z wb m4 fb s4 tb lb "
+            "m5 cb s5 G1 wl fl tl ll A1 v34 O1 cl H0 v45 H1 v56 H2 H3",
+    "sus_first": 2,
+    "waves": [(0, 4), (4, 6), (6, 7)],
+}
+
+BF, F32, I32, U16, F16 = "bfloat16", "float32", "int32", "uint16", "float16"
+SCRATCH = {
+    "win": ("sbuf", [128, DAYS * W], BF), "pay": ("sbuf", [128, DAYS * NS], BF), "sust": ("sbuf", [128, H], BF),
+    "c0": ("sbuf", [128, P], BF), "c1": ("sbuf", [128, P], BF), "pr": ("sbuf", [128, P], F16),
+    "sg": ("sbuf", [128, P], BF), "sT": ("sbuf", [128, P], BF),
+    "sc": ("sbuf", [128, P], F32), "ks": ("sbuf", [128, P], F32),
+    "half": ("sbuf", [128, P], BF), "inc": ("sbuf", [128, P], BF), "y32": ("sbuf", [128, P], F32),
+    "homeI": ("sbuf", [128, 192], I32), "awayI": ("sbuf", [128, 192], I32), "shownI": ("sbuf", [128, 56], I32),
+    "hc": ("sbuf", [128, DAYS * 96], I32), "h32": ("sbuf", [128, 96], F32),
+    "sh16": ("sbuf", [128, 56], U16), "con16": ("sbuf", [128, 192], U16), "h16": ("sbuf", [128, 96], U16),
+    "u16": ("sbuf", [128, 96], U16),
+    "rwe": ("sbuf", [128, 80], I32), "rwl": ("sbuf", [128, 48], I32),
+    "de": ("sbuf", [128, 160], BF), "dl": ("sbuf", [128, 192], BF), "db": ("sbuf", [128, 192], BF),
+    "vte": ("sbuf", [128, 160], BF), "vtl": ("sbuf", [128, 160], BF),
+    "sele": ("sbuf", [128, 128], BF), "sell": ("sbuf", [128, 64], BF),
+    "ones": ("sbuf", [128, 128], BF), "c32": ("sbuf", [128, 64], BF),
+    "idb": ("sbuf", [128, 128], BF), "idh": ("sbuf", [128, 128], F16),
+    "step": ("sbuf", [128, 256], F32), "etab": ("sbuf", [128, 32], BF), "etmp": ("sbuf", [128, 32], F32),
+    "iou": ("sbuf", [128, 32], F32), "rows": ("sbuf", [128, 128], F32), "tF": ("sbuf", [128, 128], F32),
+    "tG": ("sbuf", [128, 16], F32),
+    "pe16": ("sbuf", [128, 6], U16), "pl16": ("sbuf", [128, 4], U16), "sw16": ("sbuf", [128, 12], U16),
+    "hw": ("sbuf", [128, 96], F32),
+    "ht": ("sbuf", [128, 96], I32), "ht2": ("sbuf", [128, 96], F32), "hd": ("sbuf", [128, 96], F32),
+    "cd": ("sbuf", [128, 192], F32), "cl": ("sbuf", [128, 192], F32),
+    "pb0": ("psum", [128, 512], F32), "pb1": ("psum", [128, 512], F32), "pb2": ("psum", [128, 512], F32),
+    "pb3": ("psum", [128, 512], F32), "pb4": ("psum", [128, 512], F32), "pb5": ("psum", [128, 512], F32),
+    "pt0": ("psum", [128, 1024], BF), "pt1": ("psum", [128, 1024], BF),
+}
+SEMAPHORES = ["qv", "qs", "qt", "qg", "ldx", "ldsh", "ldhome", "ldhist", "ldaway", "ldsus", "issued", "sent", "stored",
+              "arr0", "arr1", "arr2", "arr3"]
+
+
+def rank_program(g, core, T, topo):
+    rank = T.rank_of(core)
+    if rank is None:
+        return
+    cores = list(T.cores)
+    chunks = CFG["chunks"]
+    eng = {"v": g.vector, "s": g.scalar, "t": g.tensor, "g": g, "y": g.sync}
+    known = {q: {} for q in eng}
+    count = {q: 0 for q in eng}
+    clock = {}
+    written, readers, banks = {}, {}, {}
+
+    def wait(q, tok):
+        if known[q].get(tok[0], 0) >= tok[1]:
+            return
+        eng[q].wait_ge(T.sem[tok[0]], tok[1])
+        known[q][tok[0]] = tok[1]
+        for k, v in clock.get(tok, {}).items():
+            if known[q].get(k, 0) < v:
+                known[q][k] = v
+
+    def needs(q, reads, writes):
+        deps = []
+        for n, lo, hi in reads + writes:
+            if SCRATCH[n][0] == "psum":
+                deps += [t for e, t in banks.get(n, {}).items() if e != q]
+            if q != "t" or SCRATCH[n][0] != "psum":
+                deps += [t for a, b, t in written.get(n, []) if a < hi and lo < b]
+        for n, lo, hi in writes:
+            deps += [t for a, b, t in readers.get(n, []) if a < hi and lo < b]
+        best = {}
+        for s, v in deps:
+            best[s] = max(best.get(s, 0), v)
+        for s in sorted(best, key=lambda k: k == "q" + q):
+            wait(q, (s, best[s]))
+
+    def note(q, tok, reads, writes):
+        clock[tok] = dict(known[q])
+        for n, lo, hi in reads + writes:
+            if SCRATCH[n][0] == "psum":
+                banks.setdefault(n, {})[q] = tok
+        for n, lo, hi in reads:
+            readers.setdefault(n, []).append((lo, hi, tok))
+        for n, lo, hi in writes:
+            written[n] = [w for w in written.get(n, []) if not (lo <= w[0] and w[1] <= hi)] + [(lo, hi, tok)]
+            readers[n] = [w for w in readers.get(n, []) if not (lo <= w[0] and w[1] <= hi)]
+
+    def op(q, call, reads, writes):
+        needs(q, reads, writes)
+        count[q] += 1
+        call().then_inc(T.sem["q" + q], 1)
+        note(q, ("q" + q, count[q]), reads, writes)
+
+    def A(n, lo, hi, step=1):
+        return (T[n][:, lo:hi:step] if step > 1 else T[n][:, lo:hi]), [(n, lo, hi)]
+
+    def G(win, off):
+        return win[0].indirect(off[0]), win[1] + off[1]
+
+    def copy(q, out, a):
+        if q == "v":
+            op(q, lambda: g.vector.tensor_copy(out[0], a[0]), a[1], out[1])
+        else:
+            op(q, lambda: g.scalar.activation(out[0], a[0], Act.Copy), a[1], out[1])
+
+    def tt(out, a, b, o):
+        op("v", lambda: g.vector.tensor_tensor(out[0], a[0], b[0], o), a[1] + b[1], out[1])
+
+    def ts(out, a, s1, o0, s2=None, o1=None):
+        r = list(a[1])
+        x1, x2 = s1, s2
+        if isinstance(s1, tuple):
+            x1 = s1[0]
+            r += s1[1]
+        if isinstance(s2, tuple):
+            x2 = s2[0]
+            r += s2[1]
+        if o1 is None:
+            op("v", lambda: g.vector.tensor_scalar(out[0], a[0], x1, None, o0), r, out[1])
+        else:
+            op("v", lambda: g.vector.tensor_scalar(out[0], a[0], x1, x2, o0, o1), r, out[1])
+
+    def fill(out, c):
+        op("v", lambda: g.vector.memset(out[0], c), [], out[1])
+
+    def mm(out, l, r, start, stop):
+        op("t", lambda: g.tensor.matmul(out[0], l[0], r[0], start, stop), l[1] + r[1], out[1])
+
+    def load(q, out, src, sem, total):
+        needs(q, [], out[1])
+        eng[q].dma_start(out[0], src).then_inc(T.sem[sem], 16)
+        note(q, (sem, total), [], out[1])
+
+    stores = [0]
+
+    def store(dst, a):
+        needs("y", a[1], [])
+        g.sync.dma_start(dst, a[0]).then_inc(T.sem.stored, 16)
+        stores[0] += 16
+
+    def own(d, lo=0, hi=P):
+        return A("win", d * W + lo, d * W + hi)
+
+    peers = [(rank + 1 + i) % N for i in range(N - 1)]
+    lanes = [e for e in topo.engines(core, cores[peers[0]]) if all(e in topo.engines(core, cores[q]) for q in peers)]
+    waves = CFG["waves"]
+    arrivals = sum(len(lanes) // (b - a) * (b - a) for a, b in waves)
+
+    def exchange(d):
+        for q, a, b in (("v", 0, 256), ("s", 256, 512), ("v", 512, 704), ("s", 704, NS)):
+            copy(q, A("pay", d * NS + a, d * NS + b), G(own(d), A("sh16", a // 16, b // 16)))
+        for a, b in waves:
+            needs("g", [("pay", d * NS + a * S, d * NS + b * S)], [])
+            tr, n = [], len(lanes) // (b - a)
+            for i in range(a, b):
+                q = peers[i]
+                rid, pid, _ = topo.addr(cores[q])
+                at = d * W + P + S * (rank if rank < q else rank - 1)
+                tr.append(RemoteDMATransfer(dst_ids=[DstId(rid=rid, pnc=pid)],
+                                            dma_engine_mask=sum(1 << e for e in lanes[(i - a) * n:(i - a + 1) * n]),
+                                            remote_sem=T.sem["arr%d" % d], src=T.pay[:, d * NS + i * S:d * NS + (i + 1) * S],
+                                            dst=T.win[:, at:at + S]))
+            g.remote_dma_fused(tr, local_sem=T.sem.sent)
+        note("g", ("arr%d" % d, arrivals), [], [("win", d * W + P, (d + 1) * W)])
+
+    def cols(c):
+        return c[0] * BLK, c[1] * BLK
+
+    def contact(q, d, which, a, b):
+        src = G(A("win", d * W, (d + 1) * W), A("con16", which * 96 + a // 16, which * 96 + b // 16))
+        if q == "v" and which == 1:
+            tt(A("pr", a, b), src, A("c0", a, b), Alu.add)
+        else:
+            copy(q, A("c%d" % which, a, b), src)
+
+    def turn(q, k, blocks):
+        c = chunks[k]
+        for b in blocks:
+            o = A("pb%d" % k, (b - c[0]) * BLK, (b - c[0] + 1) * BLK)
+            if q == "v":
+                mm(o, A("pr", b * BLK, (b + 1) * BLK), A("idh", 0, 128), True, True)
+            else:
+                mm(o, A("c0", b * BLK, (b + 1) * BLK), A("idb", 0, 128), True, False)
+                mm(o, A("c1", b * BLK, (b + 1) * BLK), A("idb", 0, 128), False, True)
+
+    def pressure(q, d, k, fine=False):
+        c = chunks[k]
+        contact(q, d, 0, c[0] * BLK, c[1] * BLK)
+        if fine:
+            for b in range(c[0], c[1]):
+                contact(q, d, 1, b * BLK, (b + 1) * BLK)
+                turn(q, k, [b])
+        else:
+            contact(q, d, 1, c[0] * BLK, c[1] * BLK)
+            turn(q, k, range(c[0], c[1]))
+
+    def sus_gather(q, c):
+        a, b = cols(c)
+        copy(q, A("sg", a, b), G(A("sust", 0, H), A("h16", a // 16, b // 16)))
+
+    def sus_turn(c, bank):
+        for b in range(c[0], c[1]):
+            o, i, e = A(bank, (b - c[0]) * BLK, (b - c[0] + 1) * BLK), A("sg", b * BLK, (b + 1) * BLK), A("idb", 0, 128)
+            if SCRATCH[bank][2] == F32:
+                mm(o, i, e, True, True)
+            else:
+                op("t", lambda: g.tensor.transpose(o[0], i[0], e[0]), i[1] + e[1], o[1])
+
+    def sus_copy(q, c, bank):
+        a, b = cols(c)
+        copy(q, A("sT", a, b), A(bank, 0, b - a))
+
+    def mul(k):
+        a, b = cols(chunks[k])
+        tt(A("sc", a, b), A("pb%d" % k, 0, b - a), A("sT", a, b), Alu.mult)
+
+    def scan(k):
+        a, b = cols(chunks[k])
+        o, d0, d1 = A("ks", a, b), A("step", 0, b - a), A("sc", a, b)
+        op("v", lambda: g.vector.tensor_tensor_scan(o[0], d0[0], d1[0], 0.0, Alu.add, Alu.max), d0[1] + d1[1], o[1])
+
+    part = {"e": (0, EARLY * BLK, "pe16", 5, "rwe", "de", "vte", "sele"),
+            "l": (EARLY * BLK, P, "pl16", 3, "rwl", "dl", "vtl", "sell"),
+            "a": (0, 512, "pl16", 3, "rwl", "dl", "vtl", "sell"),
+            "b": (512, 1024, "pl16", 3, "rwe", "db", "vte", "sell")}
+
+    def whole(x):
+        a, b, pl, k, r, dd, vt, sel = part[x]
+        ts(A(r, 0, 16 * k), G(A("ks", a, b), A(pl, 0, k)), float(TH + 1), Alu.max)
+
+    def frac(x):
+        a, b, pl, k, r, dd, vt, sel = part[x]
+        st = 16 * BLK // (b - a)
+        tt(A(dd, 0, 16 * k * st, st), G(A("ks", a, b), A(pl, 0, k)), A(r, 0, 16 * k), Alu.subtract)
+
+    def turn32(x):
+        a, b, pl, k, r, dd, vt, sel = part[x]
+        op("v", lambda: g.vector.transpose(T[vt][:, 0:160], T[dd][:, 0:160]), [(dd, 0, 160)], [(vt, 0, 160)])
+
+    def won(a, b):
+        return A("pb2", PF + a, PF + b)
+
+    def to_list(x):
+        a, b, pl, k, r, dd, vt, sel = part[x]
+        n = (b - a) // 16
+        for z in range(2):
+            mm(won(a // 16, b // 16), A(vt, 16 * z, 16 * z + 128), A(sel, z * n, (z + 1) * n), z == 0, z == 1)
+
+    def codes(x):
+        a, b = part[x][0] // 16, part[x][1] // 16
+        ts(A("u16", a, b), won(a, b), 1.0, Alu.add, 0.0, Alu.max)
+
+    hit, gain = A("pb3", 256, 352), A("pb3", 352, 448)
+
+    def hist_step(i, d):
+        if i == 0:
+            ts(hit, won(0, 96), 0.0, Alu.is_ge)
+        elif i == 1:
+            tt(A("hw", 0, 96), A("hd", 0, 96), won(0, 96), Alu.subtract)
+        elif i == 2:
+            tt(gain, A("hw", 0, 96), hit, Alu.mult)
+        elif i == 3:
+            o = A("h32", 0, 96) if d == DAYS - 1 else A("hc", (d + 1) * 96, (d + 2) * 96)
+            tt(o, gain, A("hc", d * 96, (d + 1) * 96), Alu.add)
+        else:
+            copy("v", A("h16", 0, 96), G(A("hc", (d + 1) * 96, (d + 2) * 96), A("sw16", 0, 6)))
+
+    def hist_ahead(i, d):
+        c = A("hc", d * 96, (d + 1) * 96)
+        if i == 0:
+            ts(A("ht", 0, 96), c, H // 16 - 1, Alu.bitwise_and)
+        elif i == 1:
+            ts(A("ht2", 0, 96), A("ht", 0, 96), 16.0, Alu.mult, 15.0, Alu.add)
+        else:
+            tt(A("hd", 0, 96), A("ht2", 0, 96), c, Alu.subtract)
+
+    def halve(q, d, a, b):
+        o, i = A("half", a, b), own(d, a, b)
+        if q == "v":
+            ts(o, i, 0.5, Alu.mult, 127.8, Alu.add)
+        else:
+            op("s", lambda: g.scalar.activation(o[0], i[0], Act.Identity, bias=T.tG[:, 14:15], scale=0.5),
+               i[1] + [("tG", 14, 15)], o[1])
+
+    def dest(d, a, b):
+        return A("y32", a, b) if d == DAYS - 1 else own(d + 1, a, b)
+
+    def done(d, a, b):
+        if d == DAYS - 1:
+            store(T.y[:, a:b], A("y32", a, b))
+
+    def renew_v(d, a, b):
+        tt(dest(d, a, b), G(A("etab", 0, 32), A("u16", a // 16, b // 16)), A("half", a, b), Alu.add)
+        done(d, a, b)
+
+    def add_half(d, j):
+        a, b = CFG["sren"][d == DAYS - 1][j]
+        mm(A("pb%d" % j, 0, b - a), A("idb", 0, 128), A("half", a, b), True, False)
+
+    def renew_gather(d, j):
+        a, b = CFG["sren"][d == DAYS - 1][j]
+        copy("s", A("inc", a, b), G(A("etab", 0, 32), A("u16", a // 16, b // 16)))
+
+    def renew_add(d, j):
+        a, b = CFG["sren"][d == DAYS - 1][j]
+        mm(A("pb%d" % j, 0, b - a), A("idb", 0, 128), A("inc", a, b), False, True)
+
+    def renew_out(d, j):
+        a, b = CFG["sren"][d == DAYS - 1][j]
+        copy("s", dest(d, a, b), A("pb%d" % j, 0, b - a))
+        done(d, a, b)
+
+    def iota(out, pattern, base):
+        op("g", lambda: g.iota(out[0], pattern, base, 0, allow_small_or_imprecise_dtypes=True), [], out[1])
+
+    load("y", own(0), T.x[:, :], "ldx", 16)
+    load("s", A("shownI", 0, 56), T.shown[:, :], "ldsh", 16)
+    load("s", A("homeI", 0, 192), T.home[:, :], "ldhome", 16)
+    load("s", A("hc", 0, 96), T.hist[:, :], "ldhist", 16)
+    for j in range(CFG["sus_first"]):
+        load("y", A("sust", j * 2048, (j + 1) * 2048), T.sus[:, j * 2048:(j + 1) * 2048], "ldsus", 64)
+    fill(A("ones", 0, 128), 1.0)
+    fill(A("tG", 14, 15), 127.8)
+    fill(A("c32", 0, 64), 32.0)
+    fill(A("step", 0, 256), 1.0 / 32)
+    fill(A("de", 0, 160), 0.0)
+    fill(A("dl", 0, 192), 0.0)
+    fill(A("db", 0, 192), 0.0)
+    fill(A("step", 0, 256, 16), -float(1 << 20))
+    iota(A("rows", 0, 16), [[1, 16]], 0)
+    iota(A("rows", 16, 32), [[2, 8], [-1, 2]], 1)
+    iota(A("iou", 0, 32), [[1, 32]], 0)
+    iota(A("rows", 32, 64), [[16, 2], [-16, 2], [128, 8]], 15)
+    iota(A("rows", 64, 80), [[32, 2], [-16, 2], [128, 4]], 15)
+    iota(A("rows", 80, 96), [[32, 2], [-16, 2], [128, 4]], 31)
+    iota(A("rows", 96, 128), [[0, 2], [-1, 16]], 16)
+    op("g", lambda: g.affine_select(T.idb[:, 0:128], T.ones[:, 0:128], [[-1, 128]], Alu.is_equal, 0.0, 0, 1),
+       [("ones", 0, 128)], [("idb", 0, 128)])
+    cut = 8 * (N - 1 - rank)
+    if cut:
+        copy("v", A("sh16", 0, cut), A("shownI", 56 - cut, 56))
+    if cut < 56:
+        copy("v", A("sh16", cut, 56), A("shownI", 0, 56 - cut))
+    exchange(0)
+    if CFG["sus_first"] < 4:
+        g.sem_inc(T.sem.issued, 1)
+        g.sync.wait_ge(T.sem.issued, 1)
+    for j in range(CFG["sus_first"], 4):
+        load("y", A("sust", j * 2048, (j + 1) * 2048), T.sus[:, j * 2048:(j + 1) * 2048], "ldsus", 64)
+    load("y", A("awayI", 0, 192), T.away[:, :], "ldaway", 16)
+    for z in range(2):
+        op("g", lambda: g.affine_select(T.sele[:, 64 * z:64 * z + 64], T.c32[:, 0:64], [[-2, 8], [-32, 4], [1000, 2]],
+                                        Alu.is_equal, 0.0, -1016 * z, 1), [("c32", 0, 64)], [("sele", 64 * z, 64 * z + 64)])
+        op("g", lambda: g.affine_select(T.sell[:, 32 * z:32 * z + 32], T.c32[:, 0:32], [[-4, 4], [-32, 4], [1000, 2]],
+                                        Alu.is_equal, 0.0, -1016 * z, 1), [("c32", 0, 32)], [("sell", 32 * z, 32 * z + 32)])
+    op("v", lambda: g.vector.transpose(T.tF[:, 0:128], T.rows[:, 0:128]), [("rows", 0, 128)], [("tF", 0, 128)])
+    copy("v", A("idh", 0, 128), A("idb", 0, 128))
+    ts(A("sw16", 0, 12), A("iou", 0, 12), 16.0, Alu.mult, A("tF", 0, 1), Alu.add)
+    hist_ahead(0, 0)
+    ts(A("tG", 0, 6), A("iou", 0, 6), 32.0, Alu.mult, A("tF", 32, 33), Alu.add)
+    ts(A("tG", 8, 12), A("iou", 0, 4), 64.0, Alu.mult, A("tF", 64, 65), Alu.add)
+    copy("v", A("con16", 0, 192), G(A("homeI", 0, 192), A("sw16", 0, 12)))
+    copy("v", A("h16", 0, 96), G(A("hc", 0, 96), A("sw16", 0, 6)))
+    hist_ahead(1, 0)
+    ts(A("etmp", 0, 32), A("iou", 0, 32), A("tF", 96, 97), Alu.is_equal, 64.0, Alu.mult)
+    halve("v", 0, 0, P)
+    ts(A("pe16", 0, 6), A("tG", 0, 6), 0.0, Alu.max, float(EARLY * BLK - 1), Alu.min)
+    ts(A("pl16", 0, 4), A("tG", 8, 12), 0.0, Alu.max, float(P - EARLY * BLK - 1), Alu.min)
+    hist_ahead(2, 0)
+    ts(A("etab", 0, 32), A("etmp", 0, 32), -128.0, Alu.add)
+
+    for d in range(DAYS):
+        last = d == DAYS - 1
+        for w in CFG["first" if d == 0 else "last" if last else "later"].split():
+            c, x = w[0], w[-1]
+            if c in "pP":
+                pressure(w[1], d, int(x), c == "P")
+            elif c == "g":
+                sus_gather(w[1], chunks[int(x)])
+            elif c == "T":
+                sus_turn(chunks[int(x)], "pt%d" % (int(x) % 2))
+            elif c == "k":
+                sus_copy(w[1], chunks[int(x)], "pt%d" % (int(x) % 2))
+            elif c == "K":
+                sus_copy("v", (4, 8), "pt1")
+            elif c == "Z":
+                halve("s", d, 768, P)
+            elif c == "d":
+                tt(A("cd", 0, 192), A("awayI", 0, 192), A("homeI", 0, 192), Alu.subtract)
+            elif c == "H":
+                hist_step(int(x), d)
+            elif c == "m":
+                mul(int(x))
+            elif c == "s":
+                scan(int(x))
+            elif c == "h":
+                add_half(d, int(x))
+            elif c == "w":
+                whole(x)
+            elif c == "f":
+                frac(x)
+            elif c == "t":
+                turn32(x)
+            elif c == "l":
+                to_list(x)
+            elif c == "c":
+                codes(x)
+            elif c == "G":
+                renew_gather(d, int(x))
+            elif c == "A":
+                renew_add(d, int(x))
+            elif c == "O":
+                renew_out(d, int(x))
+            elif c == "v":
+                renew_v(d, 256 * int(w[1]), 256 * int(w[2]))
+        if last:
+            store(T.h[:, :], A("h32", 0, 96))
+            break
+        exchange(d + 1)
+        hist_step(1, d)
+        halve("s", d + 1, 0, 768)
+        tt(A("pb4", 256, 352), A("cd", 0, 96), hit, Alu.mult)
+        hist_step(2, d)
+        tt(A("pb4", 352, 448), A("cd", 96, 192), hit, Alu.mult)
+        hist_step(3, d)
+        hist_step(4, d)
+        tt(A("cl", 0, 192), A("pb4", 256, 448), A("homeI", 0, 192), Alu.add)
+        sus_gather("s", (0, 4))
+        sus_turn((0, 4), "pb5")
+        hist_ahead(0, d + 1)
+        copy("v", A("con16", 0, 192), G(A("cl", 0, 192), A("sw16", 0, 12)))
+        sus_gather("v", (8, 12))
+        sus_gather("s", (4, 8))
+        sus_turn((8, 12), "pt0")
+        sus_turn((4, 8), "pt1")
+        sus_copy("s", (0, 4), "pb5")
+        hist_ahead(1, d + 1)
+        hist_ahead(2, d + 1)
+        sus_copy("v", (8, 12), "pt0")
+
+    for q in "vstg":
+        wait("g", ("q" + q, count[q]))
+    g.wait_ge(T.sem.sent, DAYS * arrivals)
+    g.wait_ge(T.sem.stored, stores[0])

@@ -5,59 +5,109 @@ N, P, S, H, DAYS, TH = 8, 1536, 128, 8192, 4, 7040
 W = P + (N - 1) * S
 NS = (N - 1) * S
 BLK = 128
-EARLY = 8
-PF = 384
-TAIL = "G0 G1 wl fl tl ll A0 v34 A1 O0 O1 cl H0 v46"
+PART = 4 * BLK
+LOW = 256
+LIFT = 129
 CFG = {
-    "chunks": [(0, 2), (2, 4), (4, 6), (6, 8), (8, 10), (10, 12)],
-    "sren": [[(0, 384), (384, 768)], [(256, 512), (512, 768)]],
-    "first": "ps1 pv0 ps3 pv2 ps5 pv4 gv0 d0 gs1 T0 T1 gs2 kv0 T2 gs3 m0 kv1 T3 ks2 s0 gs4 m1 T4 h0 ks3 m2 gs5 s1 T5 ks4 "
-             "s2 m3 ks5 h1 s3 we m4 fe s4 te le m5 ce s5 " + TAIL,
-    "later": "ps1 pv0 K ps2 m1 m0 h0 ps3 s1 s0 m2 ps4 s2 m3 h1 Ps5 Z s3 we m4 fe s4 te le m5 ce s5 " + TAIL,
-    "last": "ps1 pv0 K ps2 m1 m0 h0 ps3 s1 s0 wa m2 fa ps4 s2 ta la m3 ca h1 Ps5 s3 v01 G0 A0 O0 Z wb m4 fb s4 tb lb "
-            "m5 cb s5 G1 wl fl tl ll A1 v34 O1 cl H0 v45 H1 v56 H2 H3",
-    "sus_first": 2,
-    "waves": [(0, 4), (4, 6), (6, 7)],
+    "day": "pv01 ps12 pv23 ps34 kv04 kv48 ps46 m02 m24 s02 h1 s24 w04 ps68 m46 f04 m67 qv04 m78 t04 ps8a s45 s58 E0 psab m8a psbc "
+           "w48 R0 h2 s8a f48 mab A0 mbc sab sbc qs48 t48 u w8c f8c qv8c e1 t8c L0 e2 r1 O0 L1 r2 Zs45 yv02 L2 H1 ys24 H0 yvbe "
+           "H2 C0 H3 C1 ys4b X0 X1 X2 Zs04 H4 C2 gv8c T8c C3 gs07 Zv5c gs78 T08 kv8c",
+    "last": "pv01 ps12 pv23 ps34 kv04 ps46 kv48 m02 m24 nv48 h1 s04 ps68 w04 m46 f04 m67 qv04 m78 t04 s45 ps8a E0 s58 m8a nv8c w48 "
+            "psac s8a R0 h2 f48 mab A0 qs48 mbc sab sbc t48 w8c f8c qv8c e1 t8c e2 u L0 r1 L1 L2 r2 H0 O0 H1 H2 H3",
+    "first": "yv02 ys24 X0 yv48 ys8c X1 yvce X2",
+    "order": ["far", "plane", "mate"], "other": True,
+    "calls": [[(0, 1, 0, 0, 4), (1, 2, 0, 4, 8)], [(i, i + 1, 0, 2 * i - 4, 2 * i - 2) for i in range(2, 6)], [(6, 7, 0, 0, 8)]],
+    "waves": [(0, 2), (2, 6), (6, 7)],
+    "calls0": [[(0, 1, 0, 0, 4), (1, 2, 0, 4, 8)], [(i, i + 1, 0, 2 * i - 4, 2 * i - 2) for i in range(2, 6)], [(6, 7, 0, 0, 8)]],
+    "day0": "zs0c gs04 gs46 gs8c T04 T8c gv68 kv04 T48 pv01 ps12 pv23 kv8c kv48 ps34 ps46 m02 m24 h1 s02 s24 w04 ps68 m46 f04 m67 "
+            "qv04 m78 t04 ps8a s45 s58 E0 m8a psac w48 R0 h2 s8a f48 mab mbc A0 sab sbc qs48 t48 w8c f8c qv8c u e1 t8c e2 L0 r1 "
+            "O0 L1 r2 Zs45",
+    "sus_first": 4, "sus_n": 4, "sus_after": 2, "L0": "s", "probe": 0, "split": [1, 1, 1],
 }
 
-BF, F32, I32, U16, F16 = "bfloat16", "float32", "int32", "uint16", "float16"
+BF, F32, I32, U16 = "bfloat16", "float32", "int32", "uint16"
 SCRATCH = {
     "win": ("sbuf", [128, DAYS * W], BF), "pay": ("sbuf", [128, DAYS * NS], BF), "sust": ("sbuf", [128, H], BF),
-    "c0": ("sbuf", [128, P], BF), "c1": ("sbuf", [128, P], BF), "pr": ("sbuf", [128, P], F16),
-    "sg": ("sbuf", [128, P], BF), "sT": ("sbuf", [128, P], BF),
-    "sc": ("sbuf", [128, P], F32), "ks": ("sbuf", [128, P], F32),
-    "half": ("sbuf", [128, P], BF), "inc": ("sbuf", [128, P], BF), "y32": ("sbuf", [128, P], F32),
+    "cc": ("sbuf", [128, 2 * P], BF), "sg": ("sbuf", [128, P], BF), "sT": ("sbuf", [128, P], BF),
+    "inc": ("sbuf", [128, P], BF), "sc": ("sbuf", [128, P], F32), "ks": ("sbuf", [128, P], F32),
+    "half": ("sbuf", [128, (DAYS + 1) * P], BF), "y32": ("sbuf", [128, P], F32),
     "homeI": ("sbuf", [128, 192], I32), "awayI": ("sbuf", [128, 192], I32), "shownI": ("sbuf", [128, 56], I32),
-    "hc": ("sbuf", [128, DAYS * 96], I32), "h32": ("sbuf", [128, 96], F32),
+    "histI": ("sbuf", [128, 96], I32), "hc": ("sbuf", [128, (DAYS + 2) * 96], F32),
+    "near": ("sbuf", [128, 192], F32), "far": ("sbuf", [128, 192], F32),
     "sh16": ("sbuf", [128, 56], U16), "con16": ("sbuf", [128, 192], U16), "h16": ("sbuf", [128, 96], U16),
-    "u16": ("sbuf", [128, 96], U16),
-    "rwe": ("sbuf", [128, 80], I32), "rwl": ("sbuf", [128, 48], I32),
-    "de": ("sbuf", [128, 160], BF), "dl": ("sbuf", [128, 192], BF), "db": ("sbuf", [128, 192], BF),
-    "vte": ("sbuf", [128, 160], BF), "vtl": ("sbuf", [128, 160], BF),
-    "sele": ("sbuf", [128, 128], BF), "sell": ("sbuf", [128, 64], BF),
-    "ones": ("sbuf", [128, 128], BF), "c32": ("sbuf", [128, 64], BF),
-    "idb": ("sbuf", [128, 128], BF), "idh": ("sbuf", [128, 128], F16),
-    "step": ("sbuf", [128, 256], F32), "etab": ("sbuf", [128, 32], BF), "etmp": ("sbuf", [128, 32], F32),
-    "iou": ("sbuf", [128, 32], F32), "rows": ("sbuf", [128, 128], F32), "tF": ("sbuf", [128, 128], F32),
-    "tG": ("sbuf", [128, 16], F32),
-    "pe16": ("sbuf", [128, 6], U16), "pl16": ("sbuf", [128, 4], U16), "sw16": ("sbuf", [128, 12], U16),
-    "hw": ("sbuf", [128, 96], F32),
-    "ht": ("sbuf", [128, 96], I32), "ht2": ("sbuf", [128, 96], F32), "hd": ("sbuf", [128, 96], F32),
+    "top": ("sbuf", [128, 96], I32), "ft": ("sbuf", [128, 384], BF), "fT": ("sbuf", [128, 384], BF),
+    "dl": ("sbuf", [128, 160], BF), "vl": ("sbuf", [128, 160], BF), "sel": ("sbuf", [128, 192], BF),
+    "coef": ("sbuf", [128, 512], BF), "cf0": ("sbuf", [128, 512], BF), "cf1": ("sbuf", [128, 512], BF),
+    "ones": ("sbuf", [128, 128], BF), "zero": ("sbuf", [128, 128], BF), "c32": ("sbuf", [128, 32], BF), "idb": ("sbuf", [128, 128], BF),
+    "step": ("sbuf", [128, 512], F32), "iou": ("sbuf", [128, 80], F32), "rows": ("sbuf", [128, 224], F32),
+    "tF": ("sbuf", [128, 224], F32), "tG": ("sbuf", [128, 48], F32), "bias": ("sbuf", [128, 8], F32),
+    "pl16": ("sbuf", [128, 10], U16), "sw16": ("sbuf", [128, 6], U16), "sx16": ("sbuf", [128, 12], U16),
+    "un16": ("sbuf", [128, 12], U16),
+    "hw": ("sbuf", [128, 96], F32), "hq": ("sbuf", [128, 96], BF), "he": ("sbuf", [128, 96], F32),
     "cd": ("sbuf", [128, 192], F32), "cl": ("sbuf", [128, 192], F32),
     "pb0": ("psum", [128, 512], F32), "pb1": ("psum", [128, 512], F32), "pb2": ("psum", [128, 512], F32),
-    "pb3": ("psum", [128, 512], F32), "pb4": ("psum", [128, 512], F32), "pb5": ("psum", [128, 512], F32),
+    "pr0": ("psum", [128, 512], F32), "pr1": ("psum", [128, 512], F32), "pm": ("psum", [128, 512], F32),
     "pt0": ("psum", [128, 1024], BF), "pt1": ("psum", [128, 1024], BF),
 }
 SEMAPHORES = ["qv", "qs", "qt", "qg", "ldx", "ldsh", "ldhome", "ldhist", "ldaway", "ldsus", "issued", "sent", "stored",
               "arr0", "arr1", "arr2", "arr3"]
 
 
+def plan(rank, cores, topo, d):
+    core = cores[rank]
+
+    def way(q):
+        a, b = topo.chip(core), topo.chip(cores[q])
+        return CFG["order"].index("mate" if topo.mates(a, b) else "plane" if topo.same_plane(a, b) else "far")
+
+    peers = sorted([(rank + 1 + i) % N for i in range(N - 1)], key=way)
+    out = topo.engines(core, cores[peers[0]])
+    free = sorted([c for c in topo.cores_of(core) if c != core], key=lambda c: topo.die(c) == topo.die(core))
+    lanes = out + [e for e in topo.engines(core, free[0]) if e not in out]
+    calls, handed = [], {}
+    for call in CFG["calls" if d else "calls0"]:
+        calls.append([])
+        for a, b, via, lo, hi in call:
+            to = cores[peers[a]]
+            if via:
+                to = [c for c in free if c not in handed and all(topo.may_write(c, cores[q]) for q in peers[a:b])][0]
+                n = len(out) // (b - a)
+                handed[to] = [(i, i + 1, cores[peers[i]], out[(i - a) * n:(i - a + 1) * n]) for i in range(a, b)]
+            calls[-1].append((a, b, to, lanes[lo:hi]))
+    return peers, calls, handed
+
+
+def issue(g, T, topo, rank, d, call):
+    tr = []
+    for a, b, to, lanes in call:
+        src = T.pay[:, d * NS + a * S:d * NS + b * S]
+        q = T.rank_of(to)
+        at = None if q is None else d * W + P + S * (rank if rank < q else rank - 1)
+        rid, pid, _ = topo.addr(to)
+        tr.append(RemoteDMATransfer(dst_ids=[DstId(rid=rid, pnc=pid)], dma_engine_mask=sum(1 << e for e in lanes),
+                                    remote_sem=T.sem["arr%d" % d], src=src, dst=src if q is None else T.win[:, at:at + S]))
+    g.remote_dma_fused(tr, local_sem=T.sem.sent)
+
+
+def hand_on(g, core, T, topo):
+    cores = list(T.cores)
+    rank = [r for r in range(N) if topo.chip(cores[r]) == topo.chip(core)][0]
+    sent = 0
+    for d in range(DAYS):
+        peers, calls, handed = plan(rank, cores, topo, d)
+        if core in handed:
+            g.wait_ge(T.sem["arr%d" % d], sum(len(t[3]) for c in calls for t in c if t[2] == core))
+            issue(g, T, topo, rank, d, handed[core])
+            sent += sum(len(t[3]) for t in handed[core])
+    if sent:
+        g.wait_ge(T.sem.sent, sent)
+
+
 def rank_program(g, core, T, topo):
     rank = T.rank_of(core)
     if rank is None:
-        return
+        return hand_on(g, core, T, topo)
     cores = list(T.cores)
-    chunks = CFG["chunks"]
     eng = {"v": g.vector, "s": g.scalar, "t": g.tensor, "g": g, "y": g.sync}
     known = {q: {} for q in eng}
     count = {q: 0 for q in eng}
@@ -134,8 +184,20 @@ def rank_program(g, core, T, topo):
         else:
             op("v", lambda: g.vector.tensor_scalar(out[0], a[0], x1, x2, o0, o1), r, out[1])
 
+    shifts = [LOW, -LOW - 0.2, -LOW / 2 - 0.2, H * (LIFT - 0.5) + 8.0, H * LIFT + 15.0]
+
+    def affine(q, out, a, scale, k):
+        if q == "v":
+            ts(out, a, scale, Alu.mult, float(shifts[k]), Alu.add)
+        else:
+            op(q, lambda: g.scalar.activation(out[0], a[0], Act.Identity, bias=T.bias[:, k:k + 1], scale=scale),
+               a[1] + [("bias", k, k + 1)], out[1])
+
     def fill(out, c):
         op("v", lambda: g.vector.memset(out[0], c), [], out[1])
+
+    def turn32(out, a):
+        op("v", lambda: g.vector.transpose(out[0], a[0]), a[1], out[1])
 
     def mm(out, l, r, start, stop):
         op("t", lambda: g.tensor.matmul(out[0], l[0], r[0], start, stop), l[1] + r[1], out[1])
@@ -155,304 +217,275 @@ def rank_program(g, core, T, topo):
     def own(d, lo=0, hi=P):
         return A("win", d * W + lo, d * W + hi)
 
-    peers = [(rank + 1 + i) % N for i in range(N - 1)]
-    lanes = [e for e in topo.engines(core, cores[peers[0]]) if all(e in topo.engines(core, cores[q]) for q in peers)]
-    waves = CFG["waves"]
-    arrivals = sum(len(lanes) // (b - a) * (b - a) for a, b in waves)
+    ident = A("idb", 0, 128)
 
-    def exchange(d):
-        for q, a, b in (("v", 0, 256), ("s", 256, 512), ("v", 512, 704), ("s", 704, NS)):
-            copy(q, A("pay", d * NS + a, d * NS + b), G(own(d), A("sh16", a // 16, b // 16)))
-        for a, b in waves:
-            needs("g", [("pay", d * NS + a * S, d * NS + b * S)], [])
-            tr, n = [], len(lanes) // (b - a)
-            for i in range(a, b):
-                q = peers[i]
-                rid, pid, _ = topo.addr(cores[q])
-                at = d * W + P + S * (rank if rank < q else rank - 1)
-                tr.append(RemoteDMATransfer(dst_ids=[DstId(rid=rid, pnc=pid)],
-                                            dma_engine_mask=sum(1 << e for e in lanes[(i - a) * n:(i - a + 1) * n]),
-                                            remote_sem=T.sem["arr%d" % d], src=T.pay[:, d * NS + i * S:d * NS + (i + 1) * S],
-                                            dst=T.win[:, at:at + S]))
-            g.remote_dma_fused(tr, local_sem=T.sem.sent)
-        note("g", ("arr%d" % d, arrivals), [], [("win", d * W + P, (d + 1) * W)])
+    plans = [plan(rank, cores, topo, d) for d in range(DAYS)]
+    peers = plans[0][0]
+    departures = sum(len(t[3]) for p in plans for c in p[1] for t in c)
 
-    def cols(c):
-        return c[0] * BLK, c[1] * BLK
+    def show(q, d, a, b):
+        copy(q, A("pay", d * NS + a, d * NS + b), G(own(d), A("sh16", a // 16, b // 16)))
 
-    def contact(q, d, which, a, b):
-        src = G(A("win", d * W, (d + 1) * W), A("con16", which * 96 + a // 16, which * 96 + b // 16))
-        if q == "v" and which == 1:
-            tt(A("pr", a, b), src, A("c0", a, b), Alu.add)
+    def send(d, k):
+        _, calls, handed = plans[d]
+        arrivals = sum(len(t[3]) for c in calls + list(handed.values()) for t in c if t[2] in cores)
+        needs("g", [("pay", d * NS + a * S, d * NS + b * S) for a, b, _, _ in calls[k]], [])
+        issue(g, T, topo, rank, d, calls[k])
+        if d == 0 and k == CFG["sus_after"] and CFG["sus_first"] < CFG["sus_n"]:
+            g.sem_inc(T.sem.issued, 1)
+        if k == len(calls) - 1:
+            note("g", ("arr%d" % d, arrivals), [], [("win", d * W + P, (d + 1) * W)])
+
+    chunks = []
+
+    def bank(a, b):
+        k = [i for i, c in enumerate(chunks) if c[0] <= a < c[1]][0]
+        return A("pb%d" % (k % 3), a - chunks[k][0], b - chunks[k][0])
+
+    def pressure(q, d, a, b):
+        out, src = A("cc", 2 * a, 2 * b), G(A("win", d * W, (d + 1) * W), A("con16", a // 8, b // 8))
+        if d:
+            affine(q, out, src, 1.0, 0)
         else:
-            copy(q, A("c%d" % which, a, b), src)
+            copy(q, out, src)
+        for j in range(a, b, BLK):
+            for c in range(2):
+                if c and CFG["probe"]:
+                    mm(bank(j, j + BLK), A("cc", 2 * j, 2 * j + BLK), A("zero", 0, 128), False, False)
+                mm(bank(j, j + BLK), A("cc", 2 * j + c * BLK, 2 * j + (c + 1) * BLK), ident, c == 0, c == 1)
 
-    def turn(q, k, blocks):
-        c = chunks[k]
-        for b in blocks:
-            o = A("pb%d" % k, (b - c[0]) * BLK, (b - c[0] + 1) * BLK)
-            if q == "v":
-                mm(o, A("pr", b * BLK, (b + 1) * BLK), A("idh", 0, 128), True, True)
-            else:
-                mm(o, A("c0", b * BLK, (b + 1) * BLK), A("idb", 0, 128), True, False)
-                mm(o, A("c1", b * BLK, (b + 1) * BLK), A("idb", 0, 128), False, True)
+    def turned(a, b):
+        return A("pt%d" % (a // 1024), a % 1024, (b - 1) % 1024 + 1)
 
-    def pressure(q, d, k, fine=False):
-        c = chunks[k]
-        contact(q, d, 0, c[0] * BLK, c[1] * BLK)
-        if fine:
-            for b in range(c[0], c[1]):
-                contact(q, d, 1, b * BLK, (b + 1) * BLK)
-                turn(q, k, [b])
-        else:
-            contact(q, d, 1, c[0] * BLK, c[1] * BLK)
-            turn(q, k, range(c[0], c[1]))
+    def sus_turn(a, b):
+        for j in range(a, b, BLK):
+            o, i = turned(j, j + BLK), A("sg", j, j + BLK)
+            op("t", lambda: g.tensor.transpose(o[0], i[0], ident[0]), i[1] + ident[1], o[1])
 
-    def sus_gather(q, c):
-        a, b = cols(c)
-        copy(q, A("sg", a, b), G(A("sust", 0, H), A("h16", a // 16, b // 16)))
-
-    def sus_turn(c, bank):
-        for b in range(c[0], c[1]):
-            o, i, e = A(bank, (b - c[0]) * BLK, (b - c[0] + 1) * BLK), A("sg", b * BLK, (b + 1) * BLK), A("idb", 0, 128)
-            if SCRATCH[bank][2] == F32:
-                mm(o, i, e, True, True)
-            else:
-                op("t", lambda: g.tensor.transpose(o[0], i[0], e[0]), i[1] + e[1], o[1])
-
-    def sus_copy(q, c, bank):
-        a, b = cols(c)
-        copy(q, A("sT", a, b), A(bank, 0, b - a))
-
-    def mul(k):
-        a, b = cols(chunks[k])
-        tt(A("sc", a, b), A("pb%d" % k, 0, b - a), A("sT", a, b), Alu.mult)
-
-    def scan(k):
-        a, b = cols(chunks[k])
+    def scan(a, b):
         o, d0, d1 = A("ks", a, b), A("step", 0, b - a), A("sc", a, b)
         op("v", lambda: g.vector.tensor_tensor_scan(o[0], d0[0], d1[0], 0.0, Alu.add, Alu.max), d0[1] + d1[1], o[1])
 
-    part = {"e": (0, EARLY * BLK, "pe16", 5, "rwe", "de", "vte", "sele"),
-            "l": (EARLY * BLK, P, "pl16", 3, "rwl", "dl", "vtl", "sell"),
-            "a": (0, 512, "pl16", 3, "rwl", "dl", "vtl", "sell"),
-            "b": (512, 1024, "pl16", 3, "rwe", "db", "vte", "sell")}
+    def half(d, a, b):
+        return A("half", d * P + a, d * P + b)
 
-    def whole(x):
-        a, b, pl, k, r, dd, vt, sel = part[x]
-        ts(A(r, 0, 16 * k), G(A("ks", a, b), A(pl, 0, k)), float(TH + 1), Alu.max)
+    def halve(q, d, a, b):
+        affine(q, half(d, a, b), own(d, a, b), 0.5, 2 if d else 1)
 
-    def frac(x):
-        a, b, pl, k, r, dd, vt, sel = part[x]
-        st = 16 * BLK // (b - a)
-        tt(A(dd, 0, 16 * k * st, st), G(A("ks", a, b), A(pl, 0, k)), A(r, 0, 16 * k), Alu.subtract)
+    def winner(w, a, b):
+        best, top, lo, hi = A("ks", a + 15, b, 16), A("top", a // 16, b // 16), a // 4, b // 4
+        frac, square = A("ft", lo, hi, 4), A("ft", lo + 1, hi, 4)
+        if w[0] == "w":
+            ts(top, best, float(TH + 1), Alu.max)
+        elif w[0] == "f":
+            tt(frac, best, top, Alu.subtract)
+        elif w[:2] == "qv":
+            tt(square, frac, frac, Alu.mult)
+        elif w[0] == "q":
+            op("s", lambda: g.scalar.activation(square[0], frac[0], Act.Square), frac[1], square[1])
+        else:
+            turn32(A("fT", lo, hi), A("ft", lo, hi))
 
-    def turn32(x):
-        a, b, pl, k, r, dd, vt, sel = part[x]
-        op("v", lambda: g.vector.transpose(T[vt][:, 0:160], T[dd][:, 0:160]), [(dd, 0, 160)], [(vt, 0, 160)])
+    def renew(c, d, j):
+        a, b = j * PART, (j + 1) * PART
+        out, lo, hi = ("pr0", "pr1", "pb%d" % (len(chunks) % 3))[j], a // 4, b // 4
+        acc, inc = A(out, 0, PART), A("inc", a, b)
+        dh = d + (d == DAYS - 1)
+        if c == "h":
+            mm(acc, ident, half(dh, a, b), True, False)
+        elif c in "eE":
+            for i in range(4):
+                mm(A(out, i * BLK, (i + 1) * BLK), A("coef", i * BLK, (i + 1) * BLK), A("fT", lo, hi), c == "E", c == "E" or i == 3)
+        elif c == "R":
+            op("s", lambda: g.scalar.activation(inc[0], acc[0], Act.Relu), acc[1], inc[1])
+        elif c == "A":
+            mm(acc, ident, half(d, a, b), True, False)
+            mm(acc, ident, inc, False, True)
+        else:
+            n = PART // CFG["split"][j] if d == DAYS - 1 else PART
+            for i in range(0, PART, n):
+                new = own(d + 1, a, b) if d < DAYS - 1 else A("y32", a + i, a + i + n)
+                if c == "r":
+                    tt(new, A(out, i, i + n), half(dh, a + i, a + i + n), Alu.max)
+                elif d < DAYS - 1:
+                    copy("s", new, A(out, i, i + n))
+                else:
+                    affine("s", new, A(out, i, i + n), 1.0, 0)
+                if d == DAYS - 1:
+                    store(T.y[:, a + i:a + i + n], new)
 
-    def won(a, b):
-        return A("pb2", PF + a, PF + b)
+    won, lifted, hit, moved = A("pm", 0, 96), A("pm", 96, 192), A("pm", 192, 288), A("pm", 288, 480)
 
-    def to_list(x):
-        a, b, pl, k, r, dd, vt, sel = part[x]
-        n = (b - a) // 16
-        for z in range(2):
-            mm(won(a // 16, b // 16), A(vt, 16 * z, 16 * z + 128), A(sel, z * n, (z + 1) * n), z == 0, z == 1)
+    def to_list(i, q):
+        if i == 0:
+            copy(q, A("dl", 0, 160), G(A("ft", 0, 384), A("pl16", 0, 10)))
+        elif i == 1:
+            turn32(A("vl", 0, 160), A("dl", 0, 160))
+        else:
+            for out in (won, lifted):
+                if out is lifted:
+                    mm(out, ident, A("hq", 0, 96), True, False)
+                for z in range(2):
+                    mm(out, A("vl", 16 * z, 16 * z + 128), A("sel", 96 * z, 96 * z + 96), z == 0 and out is won, z == 1)
 
-    def codes(x):
-        a, b = part[x][0] // 16, part[x][1] // 16
-        ts(A("u16", a, b), won(a, b), 1.0, Alu.add, 0.0, Alu.max)
-
-    hit, gain = A("pb3", 256, 352), A("pb3", 352, 448)
+    def hist(d):
+        return A("hc", d * 96, (d + 1) * 96)
 
     def hist_step(i, d):
         if i == 0:
-            ts(hit, won(0, 96), 0.0, Alu.is_ge)
+            ts(hit, won, 0.0, Alu.is_ge)
         elif i == 1:
-            tt(A("hw", 0, 96), A("hd", 0, 96), won(0, 96), Alu.subtract)
+            tt(A("hw", 0, 96), A("he", 0, 96), lifted, Alu.subtract)
         elif i == 2:
-            tt(gain, A("hw", 0, 96), hit, Alu.mult)
-        elif i == 3:
-            o = A("h32", 0, 96) if d == DAYS - 1 else A("hc", (d + 1) * 96, (d + 2) * 96)
-            tt(o, gain, A("hc", d * 96, (d + 1) * 96), Alu.add)
+            tt(lifted if d < DAYS - 1 else A("cl", 0, 96), A("hw", 0, 96), hit, Alu.mult)
+        elif i == 4:
+            copy("v", A("h16", 0, 96), G(hist(d + 1), A("sw16", 0, 6)))
+        elif d < DAYS - 1:
+            tt(hist(d + 1), lifted, hist(d), Alu.add)
         else:
-            copy("v", A("h16", 0, 96), G(A("hc", (d + 1) * 96, (d + 2) * 96), A("sw16", 0, 6)))
+            tt(hist(d + 2), G(A("cl", 0, 96), A("un16", 0, 6)), hist(d + 1), Alu.add)
+            store(T.h[:, :], hist(d + 2))
 
-    def hist_ahead(i, d):
-        c = A("hc", d * 96, (d + 1) * 96)
-        if i == 0:
-            ts(A("ht", 0, 96), c, H // 16 - 1, Alu.bitwise_and)
-        elif i == 1:
-            ts(A("ht2", 0, 96), A("ht", 0, 96), 16.0, Alu.mult, 15.0, Alu.add)
-        else:
-            tt(A("hd", 0, 96), A("ht2", 0, 96), c, Alu.subtract)
-
-    def halve(q, d, a, b):
-        o, i = A("half", a, b), own(d, a, b)
-        if q == "v":
-            ts(o, i, 0.5, Alu.mult, 127.8, Alu.add)
-        else:
-            op("s", lambda: g.scalar.activation(o[0], i[0], Act.Identity, bias=T.tG[:, 14:15], scale=0.5),
-               i[1] + [("tG", 14, 15)], o[1])
-
-    def dest(d, a, b):
-        return A("y32", a, b) if d == DAYS - 1 else own(d + 1, a, b)
-
-    def done(d, a, b):
+    def hist_ahead(d):
         if d == DAYS - 1:
-            store(T.y[:, a:b], A("y32", a, b))
+            copy("s", hist(d + 1), G(hist(d), A("un16", 0, 6)))
+        affine("s", A("hq", 0, 96), hist(d), 16.0, 3)
+        affine("s", A("he", 0, 96), hist(d), 15.0, 4)
 
-    def renew_v(d, a, b):
-        tt(dest(d, a, b), G(A("etab", 0, 32), A("u16", a // 16, b // 16)), A("half", a, b), Alu.add)
-        done(d, a, b)
+    def contact_step(i):
+        if i < 2:
+            tt(A("pm", 288 + 96 * i, 384 + 96 * i), A("cd", 96 * i, 96 * i + 96), hit, Alu.mult)
+        elif i == 2:
+            tt(A("cl", 0, 192), moved, A("near", 0, 192), Alu.add)
+        else:
+            copy("v", A("con16", 0, 192), G(A("cl", 0, 192), A("sx16", 0, 12)))
 
-    def add_half(d, j):
-        a, b = CFG["sren"][d == DAYS - 1][j]
-        mm(A("pb%d" % j, 0, b - a), A("idb", 0, 128), A("half", a, b), True, False)
-
-    def renew_gather(d, j):
-        a, b = CFG["sren"][d == DAYS - 1][j]
-        copy("s", A("inc", a, b), G(A("etab", 0, 32), A("u16", a // 16, b // 16)))
-
-    def renew_add(d, j):
-        a, b = CFG["sren"][d == DAYS - 1][j]
-        mm(A("pb%d" % j, 0, b - a), A("idb", 0, 128), A("inc", a, b), False, True)
-
-    def renew_out(d, j):
-        a, b = CFG["sren"][d == DAYS - 1][j]
-        copy("s", dest(d, a, b), A("pb%d" % j, 0, b - a))
-        done(d, a, b)
+    def steps(text, scored):
+        chunks[:] = sorted((BLK * int(w[1], 16), BLK * int(w[2], 16)) for w in text.split() if w[0] == "m")
+        for w in text.split():
+            c, x = w[0], w[-1]
+            d = scored + (c in "yXQZ")
+            a, b = (BLK * int(w[-2], 16), BLK * int(x, 16)) if c in "pmswfqtygTkzZn" else (0, 0)
+            if c == "p":
+                pressure(w[1], d, a, b)
+            elif c == "m":
+                tt(A("sc", a, b), bank(a, b), A("sT", a, b), Alu.mult)
+            elif c == "s":
+                scan(a, b)
+            elif c in "wfqt":
+                winner(w, a, b)
+            elif c == "y":
+                show(w[1], d, a // 2, b // 2)
+            elif c == "X":
+                send(d, int(x))
+            elif c == "g":
+                copy(w[1], A("sg", a, b), G(A("sust", 0, H), A("h16", a // 16, b // 16)))
+            elif c == "T":
+                sus_turn(a, b)
+            elif c == "k":
+                copy(w[1], A("sT", a, b), turned(a, b))
+            elif c in "zZ":
+                halve(w[1], d, a, b)
+            elif c == "n":
+                affine(w[1], half(d + 1, a, b), half(d, a, b), 1.0, 0)
+            elif c in "herERAO":
+                renew(c, d, int(x))
+            elif c == "L":
+                to_list(int(x), CFG["L0"])
+            elif c == "H":
+                hist_step(int(x), scored)
+            elif c == "C":
+                contact_step(int(x))
+            elif c == "u":
+                hist_ahead(d)
 
     def iota(out, pattern, base):
         op("g", lambda: g.iota(out[0], pattern, base, 0, allow_small_or_imprecise_dtypes=True), [], out[1])
 
-    load("y", own(0), T.x[:, :], "ldx", 16)
+    def select(out, a, pattern, how, base, up):
+        op("g", lambda: g.affine_select(out[0], a[0], pattern, how, 0.0, base, up), a[1], out[1])
+
+    def load_sus(a, b):
+        n = H // CFG["sus_n"]
+        for j in range(a, b):
+            load("y", A("sust", j * n, (j + 1) * n), T.sus[:, j * n:(j + 1) * n], "ldsus", 16 * CFG["sus_n"])
+
+    def column(k):
+        return A("tF", 32 * k, 32 * k + 1)
+
     load("s", A("shownI", 0, 56), T.shown[:, :], "ldsh", 16)
+    load("y", own(0), T.x[:, :], "ldx", 16)
+    load("s", A("histI", 0, 96), T.hist[:, :], "ldhist", 16)
     load("s", A("homeI", 0, 192), T.home[:, :], "ldhome", 16)
-    load("s", A("hc", 0, 96), T.hist[:, :], "ldhist", 16)
-    for j in range(CFG["sus_first"]):
-        load("y", A("sust", j * 2048, (j + 1) * 2048), T.sus[:, j * 2048:(j + 1) * 2048], "ldsus", 64)
+    load("s", A("awayI", 0, 192), T.away[:, :], "ldaway", 16)
+    load_sus(0, CFG["sus_first"])
     fill(A("ones", 0, 128), 1.0)
-    fill(A("tG", 14, 15), 127.8)
-    fill(A("c32", 0, 64), 32.0)
-    fill(A("step", 0, 256), 1.0 / 32)
-    fill(A("de", 0, 160), 0.0)
-    fill(A("dl", 0, 192), 0.0)
-    fill(A("db", 0, 192), 0.0)
-    fill(A("step", 0, 256, 16), -float(1 << 20))
+    if CFG["probe"]:
+        fill(A("zero", 0, 128), 0.0)
+    fill(A("rows", 128, 224), 0.0)
+    fill(A("c32", 0, 32), 32.0)
+    fill(A("ft", 0, 384), 0.0)
+    for k, v in enumerate(shifts):
+        fill(A("bias", k, k + 1), float(v))
+    fill(A("rows", 130, 160, 4), -64.0)
+    fill(A("rows", 160, 192, 4), 4096.0)
+    fill(A("rows", 193, 224, 4), -65536.0)
+    fill(A("rows", 194, 224, 4), 64.0)
     iota(A("rows", 0, 16), [[1, 16]], 0)
     iota(A("rows", 16, 32), [[2, 8], [-1, 2]], 1)
-    iota(A("iou", 0, 32), [[1, 32]], 0)
-    iota(A("rows", 32, 64), [[16, 2], [-16, 2], [128, 8]], 15)
-    iota(A("rows", 64, 80), [[32, 2], [-16, 2], [128, 4]], 15)
-    iota(A("rows", 80, 96), [[32, 2], [-16, 2], [128, 4]], 31)
-    iota(A("rows", 96, 128), [[0, 2], [-1, 16]], 16)
-    op("g", lambda: g.affine_select(T.idb[:, 0:128], T.ones[:, 0:128], [[-1, 128]], Alu.is_equal, 0.0, 0, 1),
-       [("ones", 0, 128)], [("idb", 0, 128)])
-    cut = 8 * (N - 1 - rank)
-    if cut:
-        copy("v", A("sh16", 0, cut), A("shownI", 56 - cut, 56))
-    if cut < 56:
-        copy("v", A("sh16", cut, 56), A("shownI", 0, 56 - cut))
-    exchange(0)
-    if CFG["sus_first"] < 4:
-        g.sem_inc(T.sem.issued, 1)
+    iota(A("rows", 32, 48), [[2, 2], [8, 4], [1, 2]], 0)
+    iota(A("rows", 48, 64), [[2, 2], [8, 4], [-1, 2]], 1)
+    iota(A("rows", 64, 80), [[96, 2], [8, 4], [1, 2]], 0)
+    iota(A("rows", 80, 96), [[96, 2], [8, 4], [-1, 2]], 1)
+    iota(A("rows", 96, 128), [[4, 2], [32, 16]], 0)
+    for i, q in enumerate(peers):
+        k = q if q < rank else q - 1
+        copy("v", A("sh16", 8 * i, 8 * i + 8), A("shownI", 8 * k, 8 * k + 8))
+    fill(A("step", 0, 512), 1.0 / 32)
+    iota(A("iou", 0, 12), [[16, 12]], 0)
+    iota(A("iou", 16, 22), [[32, 3], [4, 2]], 0)
+    iota(A("iou", 32, 44), [[32, 3], [2, 4]], 0)
+    iota(A("iou", 48, 58), [[8, 5], [-4, 2]], 0)
+    iota(A("iou", 64, 80), [[-1, 16]], 15)
+    steps(CFG["first"], -1)
+    if CFG["sus_first"] < CFG["sus_n"]:
         g.sync.wait_ge(T.sem.issued, 1)
-    for j in range(CFG["sus_first"], 4):
-        load("y", A("sust", j * 2048, (j + 1) * 2048), T.sus[:, j * 2048:(j + 1) * 2048], "ldsus", 64)
-    load("y", A("awayI", 0, 192), T.away[:, :], "ldaway", 16)
+    load_sus(CFG["sus_first"], CFG["sus_n"])
+    select(ident, A("ones", 0, 128), [[-1, 128]], Alu.is_equal, 0, 1)
+    fill(A("step", 0, 512, 16), -float(1 << 20))
+    fill(A("ft", 2, 384, 4), 1.0)
+    turn32(A("tF", 0, 224), A("rows", 0, 224))
+    ts(A("un16", 0, 12), A("iou", 0, 12), column(0), Alu.add)
+    ts(A("sw16", 0, 6), A("iou", 16, 22), column(1), Alu.add)
+    ts(A("sx16", 0, 12), A("iou", 32, 44), column(2), Alu.add)
+    copy("v", hist(0), G(A("histI", 0, 96), A("un16", 0, 6)))
+    copy("v", A("near", 0, 192), G(A("homeI", 0, 192), A("un16", 0, 12)))
+    copy("v", A("h16", 0, 96), G(hist(0), A("sw16", 0, 6)))
+    copy("v", A("con16", 0, 192), G(A("near", 0, 192), A("sx16", 0, 12)))
+    u = A("iou", 64, 80)
+    ts(A("tG", 0, 10), A("iou", 48, 58), column(3), Alu.add)
+    ts(A("tG", 16, 32), u, column(4), Alu.mult, column(5), Alu.add)
+    ts(A("pl16", 0, 10), A("tG", 0, 10), 0.0, Alu.max, 380.0, Alu.min)
+    tt(A("tG", 32, 48), A("tG", 16, 32), u, Alu.mult)
+    ts(A("cf0", 0, 16), A("tG", 32, 48), column(6), Alu.add)
+    for n in (16, 32, 64, 128, 256):
+        copy("v", A("cf0", n, 2 * n), A("cf0", 0, n))
+    select(A("cf1", 0, 512), A("cf0", 0, 512), [[-4, 32], [0, 16]], Alu.is_ge, 0, 1)
+    select(A("coef", 0, 512), A("cf1", 0, 512), [[4, 32], [0, 16]], Alu.is_ge, 3, -1)
     for z in range(2):
-        op("g", lambda: g.affine_select(T.sele[:, 64 * z:64 * z + 64], T.c32[:, 0:64], [[-2, 8], [-32, 4], [1000, 2]],
-                                        Alu.is_equal, 0.0, -1016 * z, 1), [("c32", 0, 64)], [("sele", 64 * z, 64 * z + 64)])
-        op("g", lambda: g.affine_select(T.sell[:, 32 * z:32 * z + 32], T.c32[:, 0:32], [[-4, 4], [-32, 4], [1000, 2]],
-                                        Alu.is_equal, 0.0, -1016 * z, 1), [("c32", 0, 32)], [("sell", 32 * z, 32 * z + 32)])
-    op("v", lambda: g.vector.transpose(T.tF[:, 0:128], T.rows[:, 0:128]), [("rows", 0, 128)], [("tF", 0, 128)])
-    copy("v", A("idh", 0, 128), A("idb", 0, 128))
-    ts(A("sw16", 0, 12), A("iou", 0, 12), 16.0, Alu.mult, A("tF", 0, 1), Alu.add)
-    hist_ahead(0, 0)
-    ts(A("tG", 0, 6), A("iou", 0, 6), 32.0, Alu.mult, A("tF", 32, 33), Alu.add)
-    ts(A("tG", 8, 12), A("iou", 0, 4), 64.0, Alu.mult, A("tF", 64, 65), Alu.add)
-    copy("v", A("con16", 0, 192), G(A("homeI", 0, 192), A("sw16", 0, 12)))
-    copy("v", A("h16", 0, 96), G(A("hc", 0, 96), A("sw16", 0, 6)))
-    hist_ahead(1, 0)
-    ts(A("etmp", 0, 32), A("iou", 0, 32), A("tF", 96, 97), Alu.is_equal, 64.0, Alu.mult)
-    halve("v", 0, 0, P)
-    ts(A("pe16", 0, 6), A("tG", 0, 6), 0.0, Alu.max, float(EARLY * BLK - 1), Alu.min)
-    ts(A("pl16", 0, 4), A("tG", 8, 12), 0.0, Alu.max, float(P - EARLY * BLK - 1), Alu.min)
-    hist_ahead(2, 0)
-    ts(A("etab", 0, 32), A("etmp", 0, 32), -128.0, Alu.add)
-
-    for d in range(DAYS):
-        last = d == DAYS - 1
-        for w in CFG["first" if d == 0 else "last" if last else "later"].split():
-            c, x = w[0], w[-1]
-            if c in "pP":
-                pressure(w[1], d, int(x), c == "P")
-            elif c == "g":
-                sus_gather(w[1], chunks[int(x)])
-            elif c == "T":
-                sus_turn(chunks[int(x)], "pt%d" % (int(x) % 2))
-            elif c == "k":
-                sus_copy(w[1], chunks[int(x)], "pt%d" % (int(x) % 2))
-            elif c == "K":
-                sus_copy("v", (4, 8), "pt1")
-            elif c == "Z":
-                halve("s", d, 768, P)
-            elif c == "d":
-                tt(A("cd", 0, 192), A("awayI", 0, 192), A("homeI", 0, 192), Alu.subtract)
-            elif c == "H":
-                hist_step(int(x), d)
-            elif c == "m":
-                mul(int(x))
-            elif c == "s":
-                scan(int(x))
-            elif c == "h":
-                add_half(d, int(x))
-            elif c == "w":
-                whole(x)
-            elif c == "f":
-                frac(x)
-            elif c == "t":
-                turn32(x)
-            elif c == "l":
-                to_list(x)
-            elif c == "c":
-                codes(x)
-            elif c == "G":
-                renew_gather(d, int(x))
-            elif c == "A":
-                renew_add(d, int(x))
-            elif c == "O":
-                renew_out(d, int(x))
-            elif c == "v":
-                renew_v(d, 256 * int(w[1]), 256 * int(w[2]))
-        if last:
-            store(T.h[:, :], A("h32", 0, 96))
-            break
-        exchange(d + 1)
-        hist_step(1, d)
-        halve("s", d + 1, 0, 768)
-        tt(A("pb4", 256, 352), A("cd", 0, 96), hit, Alu.mult)
-        hist_step(2, d)
-        tt(A("pb4", 352, 448), A("cd", 96, 192), hit, Alu.mult)
-        hist_step(3, d)
-        hist_step(4, d)
-        tt(A("cl", 0, 192), A("pb4", 256, 448), A("homeI", 0, 192), Alu.add)
-        sus_gather("s", (0, 4))
-        sus_turn((0, 4), "pb5")
-        hist_ahead(0, d + 1)
-        copy("v", A("con16", 0, 192), G(A("cl", 0, 192), A("sw16", 0, 12)))
-        sus_gather("v", (8, 12))
-        sus_gather("s", (4, 8))
-        sus_turn((8, 12), "pt0")
-        sus_turn((4, 8), "pt1")
-        sus_copy("s", (0, 4), "pb5")
-        hist_ahead(1, d + 1)
-        hist_ahead(2, d + 1)
-        sus_copy("v", (8, 12), "pt0")
+        for j in range(3):
+            select(A("sel", 96 * z + 32 * j, 96 * z + 32 * j + 32), A("c32", 0, 32), [[-32, 4], [-1, 4], [1000, 2]],
+                   Alu.is_equal, -1016 * z - 4 * j, 1)
+    copy("v", A("far", 0, 192), G(A("awayI", 0, 192), A("un16", 0, 12)))
+    tt(A("cd", 0, 192), A("far", 0, 192), A("near", 0, 192), Alu.subtract)
+    day = CFG["day"].split()
+    cut = [w[0] for w in day].index("y")
+    steps(CFG["day0"] + " " + " ".join(day[cut:]), 0)
+    for d in range(1, DAYS - 1):
+        steps(CFG["day"], d)
+    steps(CFG["last"], DAYS - 1)
 
     for q in "vstg":
         wait("g", ("q" + q, count[q]))
-    g.wait_ge(T.sem.sent, DAYS * arrivals)
+    g.wait_ge(T.sem.sent, departures)
     g.wait_ge(T.sem.stored, stores[0])

from concourse.bass import DstId, RemoteDMATransfer
from concourse.mybir import AluOpType as Alu, ActivationFunctionType as Act

N, P, S, H, DAYS, TH = 8, 1536, 128, 8192, 4, 7040
W = P + (N - 1) * S
NS = (N - 1) * S
BLK = 128
PART = 4 * BLK
LOW = 256
LIFT = 129
CFG = {
    "day": "pv01 ps12 pv23 ps34 kv04 kv48 ps46 m02 m24 s02 h1 s24 w04 ps68 m46 f04 m67 qv04 m78 t04 ps8a s45 s58 E0 psab m8a psbc "
           "w48 R0 h2 s8a f48 mab A0 mbc sab sbc qs48 t48 u w8c f8c qv8c e1 t8c L0 e2 r1 O0 L1 r2 Zs45 yv02 L2 H1 ys24 H0 yvbe "
           "H2 C0 H3 C1 ys4b X0 X1 X2 Zs04 H4 C2 gv8c T8c C3 gs07 Zv5c gs78 T08 kv8c",
    "last": "pv01 ps12 pv23 ps34 kv04 ps46 kv48 m02 m24 nv48 h1 s04 ps68 w04 m46 f04 m67 qv04 m78 t04 s45 ps8a E0 s58 m8a nv8c w48 "
            "psac s8a R0 h2 f48 mab A0 qs48 mbc sab sbc t48 w8c f8c qv8c e1 t8c e2 u L0 r1 L1 L2 r2 H0 O0 H1 H2 H3",
    "first": "yv02 ys24 X0 yv48 ys8c X1 yvce X2",
    "order": ["far", "plane", "mate"], "other": True,
    "calls": [[(0, 1, 0, 0, 4), (1, 2, 0, 4, 8)], [(i, i + 1, 0, 2 * i - 4, 2 * i - 2) for i in range(2, 6)], [(6, 7, 0, 0, 8)]],
    "waves": [(0, 2), (2, 6), (6, 7)],
    "calls0": [[(0, 1, 0, 0, 4), (1, 2, 0, 4, 8)], [(i, i + 1, 0, 2 * i - 4, 2 * i - 2) for i in range(2, 6)], [(6, 7, 0, 0, 8)]],
    "day0": "zs0c gs04 gs46 gs8c T04 T8c gv68 kv04 T48 pv01 ps12 pv23 kv8c kv48 ps34 ps46 m02 m24 h1 s02 s24 w04 ps68 m46 f04 m67 "
            "qv04 m78 t04 ps8a s45 s58 E0 m8a psac w48 R0 h2 s8a f48 mab mbc A0 sab sbc qs48 t48 w8c f8c qv8c u e1 t8c e2 L0 r1 "
            "O0 L1 r2 Zs45",
    "sus_first": 4, "sus_n": 4, "sus_after": 2, "L0": "s", "probe": 0, "split": [1, 1, 1],
}

BF, F32, I32, U16 = "bfloat16", "float32", "int32", "uint16"
SCRATCH = {
    "win": ("sbuf", [128, DAYS * W], BF), "pay": ("sbuf", [128, DAYS * NS], BF), "sust": ("sbuf", [128, H], BF),
    "cc": ("sbuf", [128, 2 * P], BF), "sg": ("sbuf", [128, P], BF), "sT": ("sbuf", [128, P], BF),
    "inc": ("sbuf", [128, P], BF), "sc": ("sbuf", [128, P], F32), "ks": ("sbuf", [128, P], F32),
    "half": ("sbuf", [128, (DAYS + 1) * P], BF), "y32": ("sbuf", [128, P], F32),
    "homeI": ("sbuf", [128, 192], I32), "awayI": ("sbuf", [128, 192], I32), "shownI": ("sbuf", [128, 56], I32),
    "histI": ("sbuf", [128, 96], I32), "hc": ("sbuf", [128, (DAYS + 2) * 96], F32),
    "near": ("sbuf", [128, 192], F32), "far": ("sbuf", [128, 192], F32),
    "sh16": ("sbuf", [128, 56], U16), "con16": ("sbuf", [128, 192], U16), "h16": ("sbuf", [128, 96], U16),
    "top": ("sbuf", [128, 96], I32), "ft": ("sbuf", [128, 384], BF), "fT": ("sbuf", [128, 384], BF),
    "dl": ("sbuf", [128, 160], BF), "vl": ("sbuf", [128, 160], BF), "sel": ("sbuf", [128, 192], BF),
    "coef": ("sbuf", [128, 512], BF), "cf0": ("sbuf", [128, 512], BF), "cf1": ("sbuf", [128, 512], BF),
    "ones": ("sbuf", [128, 128], BF), "zero": ("sbuf", [128, 128], BF), "c32": ("sbuf", [128, 32], BF), "idb": ("sbuf", [128, 128], BF),
    "step": ("sbuf", [128, 512], F32), "iou": ("sbuf", [128, 80], F32), "rows": ("sbuf", [128, 224], F32),
    "tF": ("sbuf", [128, 224], F32), "tG": ("sbuf", [128, 48], F32), "bias": ("sbuf", [128, 8], F32),
    "pl16": ("sbuf", [128, 10], U16), "sw16": ("sbuf", [128, 6], U16), "sx16": ("sbuf", [128, 12], U16),
    "un16": ("sbuf", [128, 12], U16),
    "hw": ("sbuf", [128, 96], F32), "hq": ("sbuf", [128, 96], BF), "he": ("sbuf", [128, 96], F32),
    "cd": ("sbuf", [128, 192], F32), "cl": ("sbuf", [128, 192], F32),
    "pb0": ("psum", [128, 512], F32), "pb1": ("psum", [128, 512], F32), "pb2": ("psum", [128, 512], F32),
    "pr0": ("psum", [128, 512], F32), "pr1": ("psum", [128, 512], F32), "pm": ("psum", [128, 512], F32),
    "pt0": ("psum", [128, 1024], BF), "pt1": ("psum", [128, 1024], BF),
}
SEMAPHORES = ["qv", "qs", "qt", "qg", "ldx", "ldsh", "ldhome", "ldhist", "ldaway", "ldsus", "issued", "sent", "stored",
              "arr0", "arr1", "arr2", "arr3"]


def plan(rank, cores, topo, d):
    core = cores[rank]

    def way(q):
        a, b = topo.chip(core), topo.chip(cores[q])
        return CFG["order"].index("mate" if topo.mates(a, b) else "plane" if topo.same_plane(a, b) else "far")

    peers = sorted([(rank + 1 + i) % N for i in range(N - 1)], key=way)
    out = topo.engines(core, cores[peers[0]])
    free = sorted([c for c in topo.cores_of(core) if c != core], key=lambda c: topo.die(c) == topo.die(core))
    lanes = out + [e for e in topo.engines(core, free[0]) if e not in out]
    calls, handed = [], {}
    for call in CFG["calls" if d else "calls0"]:
        calls.append([])
        for a, b, via, lo, hi in call:
            to = cores[peers[a]]
            if via:
                to = [c for c in free if c not in handed and all(topo.may_write(c, cores[q]) for q in peers[a:b])][0]
                n = len(out) // (b - a)
                handed[to] = [(i, i + 1, cores[peers[i]], out[(i - a) * n:(i - a + 1) * n]) for i in range(a, b)]
            calls[-1].append((a, b, to, lanes[lo:hi]))
    return peers, calls, handed


def issue(g, T, topo, rank, d, call):
    tr = []
    for a, b, to, lanes in call:
        src = T.pay[:, d * NS + a * S:d * NS + b * S]
        q = T.rank_of(to)
        at = None if q is None else d * W + P + S * (rank if rank < q else rank - 1)
        rid, pid, _ = topo.addr(to)
        tr.append(RemoteDMATransfer(dst_ids=[DstId(rid=rid, pnc=pid)], dma_engine_mask=sum(1 << e for e in lanes),
                                    remote_sem=T.sem["arr%d" % d], src=src, dst=src if q is None else T.win[:, at:at + S]))
    g.remote_dma_fused(tr, local_sem=T.sem.sent)


def hand_on(g, core, T, topo):
    cores = list(T.cores)
    rank = [r for r in range(N) if topo.chip(cores[r]) == topo.chip(core)][0]
    sent = 0
    for d in range(DAYS):
        peers, calls, handed = plan(rank, cores, topo, d)
        if core in handed:
            g.wait_ge(T.sem["arr%d" % d], sum(len(t[3]) for c in calls for t in c if t[2] == core))
            issue(g, T, topo, rank, d, handed[core])
            sent += sum(len(t[3]) for t in handed[core])
    if sent:
        g.wait_ge(T.sem.sent, sent)


def rank_program(g, core, T, topo):
    rank = T.rank_of(core)
    if rank is None:
        return hand_on(g, core, T, topo)
    cores = list(T.cores)
    eng = {"v": g.vector, "s": g.scalar, "t": g.tensor, "g": g, "y": g.sync}
    known = {q: {} for q in eng}
    count = {q: 0 for q in eng}
    clock = {}
    written, readers, banks = {}, {}, {}

    def wait(q, tok):
        if known[q].get(tok[0], 0) >= tok[1]:
            return
        eng[q].wait_ge(T.sem[tok[0]], tok[1])
        known[q][tok[0]] = tok[1]
        for k, v in clock.get(tok, {}).items():
            if known[q].get(k, 0) < v:
                known[q][k] = v

    def needs(q, reads, writes):
        deps = []
        for n, lo, hi in reads + writes:
            if SCRATCH[n][0] == "psum":
                deps += [t for e, t in banks.get(n, {}).items() if e != q]
            if q != "t" or SCRATCH[n][0] != "psum":
                deps += [t for a, b, t in written.get(n, []) if a < hi and lo < b]
        for n, lo, hi in writes:
            deps += [t for a, b, t in readers.get(n, []) if a < hi and lo < b]
        best = {}
        for s, v in deps:
            best[s] = max(best.get(s, 0), v)
        for s in sorted(best, key=lambda k: k == "q" + q):
            wait(q, (s, best[s]))

    def note(q, tok, reads, writes):
        clock[tok] = dict(known[q])
        for n, lo, hi in reads + writes:
            if SCRATCH[n][0] == "psum":
                banks.setdefault(n, {})[q] = tok
        for n, lo, hi in reads:
            readers.setdefault(n, []).append((lo, hi, tok))
        for n, lo, hi in writes:
            written[n] = [w for w in written.get(n, []) if not (lo <= w[0] and w[1] <= hi)] + [(lo, hi, tok)]
            readers[n] = [w for w in readers.get(n, []) if not (lo <= w[0] and w[1] <= hi)]

    def op(q, call, reads, writes):
        needs(q, reads, writes)
        count[q] += 1
        call().then_inc(T.sem["q" + q], 1)
        note(q, ("q" + q, count[q]), reads, writes)

    def A(n, lo, hi, step=1):
        return (T[n][:, lo:hi:step] if step > 1 else T[n][:, lo:hi]), [(n, lo, hi)]

    def G(win, off):
        return win[0].indirect(off[0]), win[1] + off[1]

    def copy(q, out, a):
        if q == "v":
            op(q, lambda: g.vector.tensor_copy(out[0], a[0]), a[1], out[1])
        else:
            op(q, lambda: g.scalar.activation(out[0], a[0], Act.Copy), a[1], out[1])

    def tt(out, a, b, o):
        op("v", lambda: g.vector.tensor_tensor(out[0], a[0], b[0], o), a[1] + b[1], out[1])

    def ts(out, a, s1, o0, s2=None, o1=None):
        r = list(a[1])
        x1, x2 = s1, s2
        if isinstance(s1, tuple):
            x1 = s1[0]
            r += s1[1]
        if isinstance(s2, tuple):
            x2 = s2[0]
            r += s2[1]
        if o1 is None:
            op("v", lambda: g.vector.tensor_scalar(out[0], a[0], x1, None, o0), r, out[1])
        else:
            op("v", lambda: g.vector.tensor_scalar(out[0], a[0], x1, x2, o0, o1), r, out[1])

    shifts = [LOW, -LOW - 0.2, -LOW / 2 - 0.2, H * (LIFT - 0.5) + 8.0, H * LIFT + 15.0]

    def affine(q, out, a, scale, k):
        if q == "v":
            ts(out, a, scale, Alu.mult, float(shifts[k]), Alu.add)
        else:
            op(q, lambda: g.scalar.activation(out[0], a[0], Act.Identity, bias=T.bias[:, k:k + 1], scale=scale),
               a[1] + [("bias", k, k + 1)], out[1])

    def fill(out, c):
        op("v", lambda: g.vector.memset(out[0], c), [], out[1])

    def turn32(out, a):
        op("v", lambda: g.vector.transpose(out[0], a[0]), a[1], out[1])

    def mm(out, l, r, start, stop):
        op("t", lambda: g.tensor.matmul(out[0], l[0], r[0], start, stop), l[1] + r[1], out[1])

    def load(q, out, src, sem, total):
        needs(q, [], out[1])
        eng[q].dma_start(out[0], src).then_inc(T.sem[sem], 16)
        note(q, (sem, total), [], out[1])

    stores = [0]

    def store(dst, a):
        needs("y", a[1], [])
        g.sync.dma_start(dst, a[0]).then_inc(T.sem.stored, 16)
        stores[0] += 16

    def own(d, lo=0, hi=P):
        return A("win", d * W + lo, d * W + hi)

    ident = A("idb", 0, 128)

    plans = [plan(rank, cores, topo, d) for d in range(DAYS)]
    peers = plans[0][0]
    departures = sum(len(t[3]) for p in plans for c in p[1] for t in c)

    def show(q, d, a, b):
        copy(q, A("pay", d * NS + a, d * NS + b), G(own(d), A("sh16", a // 16, b // 16)))

    def send(d, k):
        _, calls, handed = plans[d]
        arrivals = sum(len(t[3]) for c in calls + list(handed.values()) for t in c if t[2] in cores)
        needs("g", [("pay", d * NS + a * S, d * NS + b * S) for a, b, _, _ in calls[k]], [])
        issue(g, T, topo, rank, d, calls[k])
        if d == 0 and k == CFG["sus_after"] and CFG["sus_first"] < CFG["sus_n"]:
            g.sem_inc(T.sem.issued, 1)
        if k == len(calls) - 1:
            note("g", ("arr%d" % d, arrivals), [], [("win", d * W + P, (d + 1) * W)])

    chunks = []

    def bank(a, b):
        k = [i for i, c in enumerate(chunks) if c[0] <= a < c[1]][0]
        return A("pb%d" % (k % 3), a - chunks[k][0], b - chunks[k][0])

    def pressure(q, d, a, b):
        out, src = A("cc", 2 * a, 2 * b), G(A("win", d * W, (d + 1) * W), A("con16", a // 8, b // 8))
        if d:
            affine(q, out, src, 1.0, 0)
        else:
            copy(q, out, src)
        for j in range(a, b, BLK):
            for c in range(2):
                if c and CFG["probe"]:
                    mm(bank(j, j + BLK), A("cc", 2 * j, 2 * j + BLK), A("zero", 0, 128), False, False)
                mm(bank(j, j + BLK), A("cc", 2 * j + c * BLK, 2 * j + (c + 1) * BLK), ident, c == 0, c == 1)

    def turned(a, b):
        return A("pt%d" % (a // 1024), a % 1024, (b - 1) % 1024 + 1)

    def sus_turn(a, b):
        for j in range(a, b, BLK):
            o, i = turned(j, j + BLK), A("sg", j, j + BLK)
            op("t", lambda: g.tensor.transpose(o[0], i[0], ident[0]), i[1] + ident[1], o[1])

    def scan(a, b):
        o, d0, d1 = A("ks", a, b), A("step", 0, b - a), A("sc", a, b)
        op("v", lambda: g.vector.tensor_tensor_scan(o[0], d0[0], d1[0], 0.0, Alu.add, Alu.max), d0[1] + d1[1], o[1])

    def half(d, a, b):
        return A("half", d * P + a, d * P + b)

    def halve(q, d, a, b):
        affine(q, half(d, a, b), own(d, a, b), 0.5, 2 if d else 1)

    def winner(w, a, b):
        best, top, lo, hi = A("ks", a + 15, b, 16), A("top", a // 16, b // 16), a // 4, b // 4
        frac, square = A("ft", lo, hi, 4), A("ft", lo + 1, hi, 4)
        if w[0] == "w":
            ts(top, best, float(TH + 1), Alu.max)
        elif w[0] == "f":
            tt(frac, best, top, Alu.subtract)
        elif w[:2] == "qv":
            tt(square, frac, frac, Alu.mult)
        elif w[0] == "q":
            op("s", lambda: g.scalar.activation(square[0], frac[0], Act.Square), frac[1], square[1])
        else:
            turn32(A("fT", lo, hi), A("ft", lo, hi))

    def renew(c, d, j):
        a, b = j * PART, (j + 1) * PART
        out, lo, hi = ("pr0", "pr1", "pb%d" % (len(chunks) % 3))[j], a // 4, b // 4
        acc, inc = A(out, 0, PART), A("inc", a, b)
        dh = d + (d == DAYS - 1)
        if c == "h":
            mm(acc, ident, half(dh, a, b), True, False)
        elif c in "eE":
            for i in range(4):
                mm(A(out, i * BLK, (i + 1) * BLK), A("coef", i * BLK, (i + 1) * BLK), A("fT", lo, hi), c == "E", c == "E" or i == 3)
        elif c == "R":
            op("s", lambda: g.scalar.activation(inc[0], acc[0], Act.Relu), acc[1], inc[1])
        elif c == "A":
            mm(acc, ident, half(d, a, b), True, False)
            mm(acc, ident, inc, False, True)
        else:
            n = PART // CFG["split"][j] if d == DAYS - 1 else PART
            for i in range(0, PART, n):
                new = own(d + 1, a, b) if d < DAYS - 1 else A("y32", a + i, a + i + n)
                if c == "r":
                    tt(new, A(out, i, i + n), half(dh, a + i, a + i + n), Alu.max)
                elif d < DAYS - 1:
                    copy("s", new, A(out, i, i + n))
                else:
                    affine("s", new, A(out, i, i + n), 1.0, 0)
                if d == DAYS - 1:
                    store(T.y[:, a + i:a + i + n], new)

    won, lifted, hit, moved = A("pm", 0, 96), A("pm", 96, 192), A("pm", 192, 288), A("pm", 288, 480)

    def to_list(i, q):
        if i == 0:
            copy(q, A("dl", 0, 160), G(A("ft", 0, 384), A("pl16", 0, 10)))
        elif i == 1:
            turn32(A("vl", 0, 160), A("dl", 0, 160))
        else:
            for out in (won, lifted):
                if out is lifted:
                    mm(out, ident, A("hq", 0, 96), True, False)
                for z in range(2):
                    mm(out, A("vl", 16 * z, 16 * z + 128), A("sel", 96 * z, 96 * z + 96), z == 0 and out is won, z == 1)

    def hist(d):
        return A("hc", d * 96, (d + 1) * 96)

    def hist_step(i, d):
        if i == 0:
            ts(hit, won, 0.0, Alu.is_ge)
        elif i == 1:
            tt(A("hw", 0, 96), A("he", 0, 96), lifted, Alu.subtract)
        elif i == 2:
            tt(lifted if d < DAYS - 1 else A("cl", 0, 96), A("hw", 0, 96), hit, Alu.mult)
        elif i == 4:
            copy("v", A("h16", 0, 96), G(hist(d + 1), A("sw16", 0, 6)))
        elif d < DAYS - 1:
            tt(hist(d + 1), lifted, hist(d), Alu.add)
        else:
            tt(hist(d + 2), G(A("cl", 0, 96), A("un16", 0, 6)), hist(d + 1), Alu.add)
            store(T.h[:, :], hist(d + 2))

    def hist_ahead(d):
        if d == DAYS - 1:
            copy("s", hist(d + 1), G(hist(d), A("un16", 0, 6)))
        affine("s", A("hq", 0, 96), hist(d), 16.0, 3)
        affine("s", A("he", 0, 96), hist(d), 15.0, 4)

    def contact_step(i):
        if i < 2:
            tt(A("pm", 288 + 96 * i, 384 + 96 * i), A("cd", 96 * i, 96 * i + 96), hit, Alu.mult)
        elif i == 2:
            tt(A("cl", 0, 192), moved, A("near", 0, 192), Alu.add)
        else:
            copy("v", A("con16", 0, 192), G(A("cl", 0, 192), A("sx16", 0, 12)))

    def steps(text, scored):
        chunks[:] = sorted((BLK * int(w[1], 16), BLK * int(w[2], 16)) for w in text.split() if w[0] == "m")
        for w in text.split():
            c, x = w[0], w[-1]
            d = scored + (c in "yXQZ")
            a, b = (BLK * int(w[-2], 16), BLK * int(x, 16)) if c in "pmswfqtygTkzZn" else (0, 0)
            if c == "p":
                pressure(w[1], d, a, b)
            elif c == "m":
                tt(A("sc", a, b), bank(a, b), A("sT", a, b), Alu.mult)
            elif c == "s":
                scan(a, b)
            elif c in "wfqt":
                winner(w, a, b)
            elif c == "y":
                show(w[1], d, a // 2, b // 2)
            elif c == "X":
                send(d, int(x))
            elif c == "g":
                copy(w[1], A("sg", a, b), G(A("sust", 0, H), A("h16", a // 16, b // 16)))
            elif c == "T":
                sus_turn(a, b)
            elif c == "k":
                copy(w[1], A("sT", a, b), turned(a, b))
            elif c in "zZ":
                halve(w[1], d, a, b)
            elif c == "n":
                affine(w[1], half(d + 1, a, b), half(d, a, b), 1.0, 0)
            elif c in "herERAO":
                renew(c, d, int(x))
            elif c == "L":
                to_list(int(x), CFG["L0"])
            elif c == "H":
                hist_step(int(x), scored)
            elif c == "C":
                contact_step(int(x))
            elif c == "u":
                hist_ahead(d)

    def iota(out, pattern, base):
        op("g", lambda: g.iota(out[0], pattern, base, 0, allow_small_or_imprecise_dtypes=True), [], out[1])

    def select(out, a, pattern, how, base, up):
        op("g", lambda: g.affine_select(out[0], a[0], pattern, how, 0.0, base, up), a[1], out[1])

    def load_sus(a, b):
        n = H // CFG["sus_n"]
        for j in range(a, b):
            load("y", A("sust", j * n, (j + 1) * n), T.sus[:, j * n:(j + 1) * n], "ldsus", 16 * CFG["sus_n"])

    def column(k):
        return A("tF", 32 * k, 32 * k + 1)

    load("s", A("shownI", 0, 56), T.shown[:, :], "ldsh", 16)
    load("y", own(0), T.x[:, :], "ldx", 16)
    load("s", A("histI", 0, 96), T.hist[:, :], "ldhist", 16)
    load("s", A("homeI", 0, 192), T.home[:, :], "ldhome", 16)
    load("s", A("awayI", 0, 192), T.away[:, :], "ldaway", 16)
    load_sus(0, CFG["sus_first"])
    fill(A("ones", 0, 128), 1.0)
    if CFG["probe"]:
        fill(A("zero", 0, 128), 0.0)
    fill(A("rows", 128, 224), 0.0)
    fill(A("c32", 0, 32), 32.0)
    fill(A("ft", 0, 384), 0.0)
    for k, v in enumerate(shifts):
        fill(A("bias", k, k + 1), float(v))
    fill(A("rows", 130, 160, 4), -64.0)
    fill(A("rows", 160, 192, 4), 4096.0)
    fill(A("rows", 193, 224, 4), -65536.0)
    fill(A("rows", 194, 224, 4), 64.0)
    iota(A("rows", 0, 16), [[1, 16]], 0)
    iota(A("rows", 16, 32), [[2, 8], [-1, 2]], 1)
    iota(A("rows", 32, 48), [[2, 2], [8, 4], [1, 2]], 0)
    iota(A("rows", 48, 64), [[2, 2], [8, 4], [-1, 2]], 1)
    iota(A("rows", 64, 80), [[96, 2], [8, 4], [1, 2]], 0)
    iota(A("rows", 80, 96), [[96, 2], [8, 4], [-1, 2]], 1)
    iota(A("rows", 96, 128), [[4, 2], [32, 16]], 0)
    for i, q in enumerate(peers):
        k = q if q < rank else q - 1
        copy("v", A("sh16", 8 * i, 8 * i + 8), A("shownI", 8 * k, 8 * k + 8))
    fill(A("step", 0, 512), 1.0 / 32)
    iota(A("iou", 0, 12), [[16, 12]], 0)
    iota(A("iou", 16, 22), [[32, 3], [4, 2]], 0)
    iota(A("iou", 32, 44), [[32, 3], [2, 4]], 0)
    iota(A("iou", 48, 58), [[8, 5], [-4, 2]], 0)
    iota(A("iou", 64, 80), [[-1, 16]], 15)
    steps(CFG["first"], -1)
    if CFG["sus_first"] < CFG["sus_n"]:
        g.sync.wait_ge(T.sem.issued, 1)
    load_sus(CFG["sus_first"], CFG["sus_n"])
    select(ident, A("ones", 0, 128), [[-1, 128]], Alu.is_equal, 0, 1)
    fill(A("step", 0, 512, 16), -float(1 << 20))
    fill(A("ft", 2, 384, 4), 1.0)
    turn32(A("tF", 0, 224), A("rows", 0, 224))
    ts(A("un16", 0, 12), A("iou", 0, 12), column(0), Alu.add)
    ts(A("sw16", 0, 6), A("iou", 16, 22), column(1), Alu.add)
    ts(A("sx16", 0, 12), A("iou", 32, 44), column(2), Alu.add)
    copy("v", hist(0), G(A("histI", 0, 96), A("un16", 0, 6)))
    copy("v", A("near", 0, 192), G(A("homeI", 0, 192), A("un16", 0, 12)))
    copy("v", A("h16", 0, 96), G(hist(0), A("sw16", 0, 6)))
    copy("v", A("con16", 0, 192), G(A("near", 0, 192), A("sx16", 0, 12)))
    u = A("iou", 64, 80)
    ts(A("tG", 0, 10), A("iou", 48, 58), column(3), Alu.add)
    ts(A("tG", 16, 32), u, column(4), Alu.mult, column(5), Alu.add)
    ts(A("pl16", 0, 10), A("tG", 0, 10), 0.0, Alu.max, 380.0, Alu.min)
    tt(A("tG", 32, 48), A("tG", 16, 32), u, Alu.mult)
    ts(A("cf0", 0, 16), A("tG", 32, 48), column(6), Alu.add)
    for n in (16, 32, 64, 128, 256):
        copy("v", A("cf0", n, 2 * n), A("cf0", 0, n))
    select(A("cf1", 0, 512), A("cf0", 0, 512), [[-4, 32], [0, 16]], Alu.is_ge, 0, 1)
    select(A("coef", 0, 512), A("cf1", 0, 512), [[4, 32], [0, 16]], Alu.is_ge, 3, -1)
    for z in range(2):
        for j in range(3):
            select(A("sel", 96 * z + 32 * j, 96 * z + 32 * j + 32), A("c32", 0, 32), [[-32, 4], [-1, 4], [1000, 2]],
                   Alu.is_equal, -1016 * z - 4 * j, 1)
    copy("v", A("far", 0, 192), G(A("awayI", 0, 192), A("un16", 0, 12)))
    tt(A("cd", 0, 192), A("far", 0, 192), A("near", 0, 192), Alu.subtract)
    day = CFG["day"].split()
    cut = [w[0] for w in day].index("y")
    steps(CFG["day0"] + " " + " ".join(day[cut:]), 0)
    for d in range(1, DAYS - 1):
        steps(CFG["day"], d)
    steps(CFG["last"], DAYS - 1)

    for q in "vstg":
        wait("g", ("q" + q, count[q]))
    g.wait_ge(T.sem.sent, departures)
    g.wait_ge(T.sem.stored, stores[0])
